import numpy as np, ml_dtypes
CORES = [35,38,43,46]
N = 4
import mx_ref
BF = ml_dtypes.bfloat16
def gentries(a):
    return np.ascontiguousarray(a.reshape(8, 16, -1).transpose(0, 2, 1)).reshape(8, -1)
def gtable(e):
    e = np.asarray(e); return np.ascontiguousarray(e.reshape(8, -1, 16).transpose(0, 2, 1)).reshape(128, -1).astype(np.int32)
def gcols(t, e):
    v = np.concatenate([t.reshape(8, 16, -1, 4), np.zeros((8, 16, 1, 4), BF)], axis=2)
    return np.ascontiguousarray(np.stack([v[g][:, e[g]] for g in range(8)])).reshape(128, -1)
def tile(rs):
    return np.stack(rs, axis=2).reshape(128, -1).astype(BF)
def pick(q, e):
    c = np.concatenate([q[0].reshape(128, -1, 4), np.zeros((128, 1, 4), np.uint8)], axis=1); s = np.concatenate([q[1], np.ones((16, 1), np.uint8)], axis=1)
    return (np.ascontiguousarray(c[:, e].reshape(128, -1)), np.ascontiguousarray(s[:, e]))
def join(*qs):
    return (np.concatenate([q[0] for q in qs], axis=1), np.concatenate([q[1] for q in qs], axis=1))
def put(q, e, v):
    c, s = q[0].reshape(128, -1, 4).copy(), q[1].copy(); c[:, e] = v[0].reshape(128, -1, 4); s[:, e] = v[1]
    return (c.reshape(128, -1), s)
def pk(c, s):
    return (np.ascontiguousarray(c), mx_ref.live(s))
def emit(q):
    return q[0], q[1]
def packed(v, rng):
    q = [mx_ref.quantize(np.ascontiguousarray(v[r])) for r in range(N)]
    return np.stack([a for a, b in q]), np.stack([mx_ref.plane(b, rng) for a, b in q])
def f(rng, *shape):
    return mx_ref.flush((rng.standard_normal(shape, dtype=np.float32) * np.exp2(rng.integers(-2, 3, shape[:-1] + (1,)))).astype(BF))
def wide(rng, *shape, cols=0):
    v = rng.standard_normal(shape, dtype=np.float32) * np.exp2(rng.integers(-12, 13, shape)).astype(np.float32)
    if cols: v *= np.repeat(np.exp2(rng.integers(-cols, cols + 1, shape[:-2] + (1, shape[-1] // 4))) * (rng.random(shape[:-2] + (1, shape[-1] // 4)) > 0.0625), 4, axis=-1).astype(np.float32)
    return mx_ref.flush(v.astype(BF))
C, R = 512, 2
def partners(rng, n):
    e = np.tile(np.arange(C), (N, 8, 1))
    p = rng.permuted(e, axis=2)
    k, m = p[:, :, :n], p[:, :, n:2 * n]
    np.put_along_axis(e, k, m, axis=2)
    np.put_along_axis(e, m, k, axis=2)
    return e
def stored(e):
    return np.stack([gtable(e[r]) for r in range(N)])
def layers(rng, v, w):
    (a, b), (c, d) = packed(v, rng), packed(w, rng)
    return {"vc": a, "vs": b, "wc": c, "ws": d}
def units(rng, kv, kw):
    w = np.zeros((N, 128, 4, 128, 4), np.float32)
    i = np.arange(128)
    for b in range(4): w[:, i, b, i, b] = 1
    w = w.reshape(N, 128, 2048)
    return layers(rng, *[(w * np.reshape(k, (N, 1, 1)).astype(np.float32) + np.float32(0.0)).astype(BF) for k in (kv, kw)])
def moves_alone(rng):
    k = rng.permutation(N) % 2 * 32.0
    return units(rng, k, 32.0 - k)
def setup_inputs(rng):
    return {"x": np.array(f(rng, N, 128, 4 * C)), "pr": stored(partners(rng, int(rng.integers(3 * C // 8, C // 2 + 1)))), "u": np.array(f(rng, N, 128, 512)), "a": np.array(f(rng, N, 128, 512)), **layers(rng, f(rng, N, 128, 2048), f(rng, N, 128, 2048))}
def setup_inputs_rest(rng):
    d = setup_inputs(rng)
    e = partners(rng, C // 2)
    o = rng.permutation(N)
    d["x"][o[0]] = 0
    e[o[1]] = np.arange(C)
    d["pr"] = stored(e)
    return d
def setup_inputs_near(rng):
    d = setup_inputs(rng)
    e = partners(rng, C // 2)
    j = np.arange(C)
    n = np.cumsum(e > j, axis=2) - 1
    n = np.take_along_axis(n, np.minimum(e, j), axis=2)
    flip = np.take_along_axis(rng.integers(0, 2, (N, 8, C // 2)), n, axis=2) > 0
    h = np.take_along_axis(rng.integers(-3, 4, (N, 8, C // 2)), n, axis=2)
    first = (e > j) ^ flip
    kind = n % 9
    plus = np.where(kind == 7, True, np.where(kind == 8, False, first))
    m = np.where(first, h, kind - 3 - h)
    size = np.exp2(np.arange(4) - 23.0)
    x = np.zeros((N, 8, 16, C, 4), np.float32)
    x[:, :, 0, :, 0] = plus
    x[:, :, 1, :, 0] = ~plus
    x[:, :, 2:8] = rng.integers(4, 8, (N, 8, 6, C, 4)) * 0.125
    x[:, :, 8] = ((np.maximum(m, 0)[..., None] >> np.arange(4)) & 1) * size
    x[:, :, 9] = ((np.maximum(-m, 0)[..., None] >> np.arange(4)) & 1) * size
    x[:, :, 10:] = rng.integers(4, 8, (N, 8, 6, C, 4)) * 2.0 ** -20
    u = np.zeros((N, 128, 8, 4), np.float32)
    for g in range(8):
        u[:, 16 * g, g, 0] = 1
        u[:, 16 * g + 1, g, 0] = -1
        u[:, 16 * g + 8, g] = 1
        u[:, 16 * g + 9, g] = -1
    z = rng.permutation(N) % 3 - 1.0
    x = x * np.exp2(7 * z).reshape(N, 1, 1, 1, 1)
    u = u * np.exp2(30 * z).reshape(N, 1, 1, 1) + 0.0
    d["x"] = x.astype(np.float32).reshape(N, 128, 4 * C).astype(BF)
    d["pr"] = stored(e)
    d["u"].reshape(N, 128, 128, 4)[:, :, ::16] = u.astype(np.float32).astype(BF)
    return {**d, **moves_alone(rng)}
def setup_inputs_huge(rng):
    d = setup_inputs(rng)
    x = 2.0 ** 30 * (0.6 + 0.4 * rng.random((N, 128, C, 4)))
    s = np.stack([rng.permutation(8) % 2 * 2.0 - 1.0 for r in range(N)])
    o = rng.permutation(N)
    s[o[0]] = 1
    s[o[1]] = -1
    g = np.ones((N, 128, 8)) * s[:, None, :]
    for r in o[2::2]:
        g[r, 64:] *= -1
        c = rng.permutation(C) % 2 == 0
        x[r, :64] *= np.where(c, 1.0, 2.0 ** -20)[None, :, None]
        x[r, 64:] *= np.where(c, 2.0 ** -20, 1.0)[None, :, None]
    u = 2.0 ** 30 * (1 - 0.25 * rng.random((N, 128, 8, 4))) * g[..., None]
    d["x"] = x.astype(np.float32).reshape(N, 128, 4 * C).astype(BF)
    d["pr"] = stored(partners(rng, C // 2))
    d["u"].reshape(N, 128, 128, 4)[:, :, ::16] = u.astype(np.float32).astype(BF)
    return {**d, **moves_alone(rng)}
def setup_inputs_flip(rng):
    d = setup_inputs(rng)
    x = (1 + rng.random((N, 128, C, 4))) * np.exp2(rng.integers(24, 29, (N, 1, C, 1)))
    u = (1 + rng.random((N, 128, 8, 4))) * (rng.permutation(N) % 2 * 2.0 - 1.0).reshape(N, 1, 1, 1)
    d["x"] = x.astype(np.float32).reshape(N, 128, 4 * C).astype(BF)
    d["pr"] = stored(partners(rng, C // 2))
    d["u"].reshape(N, 128, 128, 4)[:, :, ::16] = u.astype(np.float32).astype(BF)
    return {**d, **units(rng, np.full(N, -32.0), np.full(N, -32.0))}
def setup_inputs_spread(rng):
    d = setup_inputs(rng)
    d["x"] = wide(rng, N, 128, 4 * C, cols=6)
    return d
def check_inputs(d):
    b = []
    for k in ("x", "u", "a"):
        v = np.abs(d[k].astype(np.float32))
        if not (np.isfinite(v).all() and ((v == 0) | (v >= 2.0 ** -30) & (v <= 2.0 ** 30)).all()): b.append("a value of " + k)
    e = np.stack([gentries(p) for p in d["pr"]])
    if ((e < 0) | (e >= C)).any(): b.append("an entry of pr is out of range")
    elif (np.take_along_axis(e, e, axis=2) != np.arange(C)).any(): b.append("a column isn't its partner's partner")
    for k in ("v", "w"):
        c = d[k + "c"] & 127
        s = np.stack([mx_ref.live(p) for p in d[k + "s"]]).astype(int)
        if (c == 127).any(): b.append("a code of " + k + "c isn't a number")
        full = c.reshape(N, 16, 8, 512, 4).any(axis=(2, 4))
        if ((s > 157) | full & (s < 80)).any(): b.append("a scale of " + k + "s is out of range")
    return b
def reference(x, pr, u, a, vc, vs, wc, ws):
    partner = [gentries(pr[r]) for r in range(N)]
    qu = [mx_ref.quantize(u[r]) for r in range(N)]
    lv, lw = [pk(vc[r], vs[r]) for r in range(N)], [pk(wc[r], ws[r]) for r in range(N)]
    four = [np.arange(128 * b, 128 * b + 128) for b in range(4)]
    now = [x[r] for r in range(N)]
    last = np.zeros((N, 8, C), int)
    for t in range(R):
        start = np.arange(C)
        q = []
        for r in range(N):
            s = mx_ref.matmul(qu[r], mx_ref.quantize(now[r]))[::16]
            c = np.where(s + np.take_along_axis(s, partner[r], axis=1) > 0, partner[r], np.arange(C))
            l = [c[0]]
            for g in range(1, 8): l.append(c[g][l[g - 1]])
            l = np.stack(l)
            last[r] = l[:, start]
            q.append(mx_ref.quantize(gcols(now[r], last[r])))
            start = l[7][start]
        now = [tile([np.maximum(mx_ref.matmul(pick(lv[r], k), q[r]), mx_ref.matmul(pick(lw[r], k), q[(r - 1) % N])) * np.float32(0.03125) for k in four]) for r in range(N)]
    y, ol = np.zeros((N, 128, C), np.float32), np.zeros((N, 8, C), np.float32)
    oc, osc = np.zeros((N, 128, 4 * C), np.uint8), np.zeros((N, 16, C), np.uint8)
    for r in range(N):
        z = mx_ref.quantize(now[r])
        y[r] = mx_ref.matmul(mx_ref.quantize(a[r]), z)
        ol[r] = last[r]
        oc[r], osc[r] = emit(z)
    return {"y": y, "ol": ol, "oc": oc, "osc": osc}

@@ -1,0 +1,484 @@
+from concourse.bass import DstId, RemoteDMATransfer
+from concourse.mybir import dt, AluOpType, ActivationFunctionType
+
+C = 512
+R = 2
+H = C // 2
+SC = 0.03125
+BIG = 2.0 ** 96
+LT = "float16"
+X4 = "float8_e4m3fn_x4"
+CFG = {"calls": (4, 4, 4, 3), "cut": (128, 256)}
+
+
+def _scratch():
+    s = {}
+
+    def sb(n, w, d):
+        s[n] = ("sbuf", [128, w], d)
+    for n in ("ub", "ab"):
+        sb(n, 512, "bfloat16")
+    for n in ("uq", "uq2", "aq"):
+        sb(n, 128, X4)
+    for n in ("us", "us2", "asc"):
+        sb(n, 128, "uint8")
+    for n in ("vq", "wq"):
+        sb(n, C, X4)
+    for n in ("vp", "wp"):
+        sb(n, C, "uint8")
+    sb("pri", 32, "int32"); sb("pro", 32, "uint16"); sb("dd", 32, "float32")
+    sb("pcol", 2, "int32"); sb("pand", 2, "int32"); sb("pm", 2, "float32")
+    sb("k16", 32, "float32"); sb("jw", 32, "float32"); sb("uoff", 8, "uint16")
+    sb("jm", C, "float32"); sb("row", C, "float32"); sb("mbig", C, "float32")
+    sb("mask", C, "bfloat16"); sb("rst", C, "bfloat16")
+    sb("sv", C, "float32"); sb("thr", C, "float32"); sb("vb", C, "bfloat16"); sb("wb", C, "bfloat16")
+    sb("t1", 32, "float32"); sb("cw", 32, "float32"); sb("o0", 32, "uint16"); sb("o4", 32, "uint16")
+    sb("asm", 96, "float32"); sb("bt", 96, "float32"); sb("ou", 96, "uint16")
+    for n in ("ta", "tb", "t7", "t8", "t9", "la", "lb", "ysb"):
+        sb(n, C, "float32")
+    for n in ("tm", "ts", "tm2", "ts2", "tm4", "ts4"):
+        sb(n, C, LT)
+    sb("sa", 32, LT); sb("sc", 32, LT)
+    for t in range(R + 1):
+        sb("x%d" % t, 4 * C, "bfloat16"); sb("xq%d" % t, C, X4); sb("xs%d" % t, C, "uint8")
+    for t in range(R):
+        sb("off%d" % t, 128, "uint16"); sb("lr%d" % t, 96, "uint16"); sb("bw%d" % t, 32, "uint16")
+        sb("yt%d" % t, 4 * C, "bfloat16")
+        for n in ("y", "z", "k"):
+            sb("%sq%d" % (n, t), C, X4); sb("%sp%d" % (n, t), C, "uint8")
+        sb("av%d" % t, 4 * C, "float32"); sb("mx%d" % t, 4 * C, "float32")
+    for b in range(8):
+        s["ps%d" % b] = ("psum", [128, 512], "float32")
+    return s
+
+
+SCRATCH = _scratch()
+SEMAPHORES = (["cv", "ca", "cp", "cg", "sent", "outs"] + ["ld%d" % i for i in range(9)]
+              + ["lst%d_%d" % (t, k) for t in range(R) for k in range(3)] + ["dat%d_%d" % (t, h) for t in range(R) for h in range(2)])
+
+
+def _list_masks(topo, src, dsts):
+    eng = {d: topo.engines(src, d) for d in dsts}
+    few = min(len(e) for e in eng.values())
+    narrow = [d for d in dsts if len(eng[d]) == few]
+    used, out = set(), {}
+    for d in narrow + [d for d in dsts if d not in narrow]:
+        free = [e for e in eng[d] if e not in used]
+        want = few // len(narrow) if d in narrow else len(free)
+        n = 1
+        while 2 * n <= min(want, len(free)):
+            n *= 2
+        used.update(free[:n])
+        out[d] = free[:n]
+    return out
+
+
+def rank_program(g, core, T, topo):
+    r = T.rank_of(core)
+    if r is None:
+        return
+    cores = T.cores
+    N = len(cores)
+    Q = {"v": g.vector, "a": g.scalar, "p": g.tensor, "s": g.sync, "g": g}
+    CS = {"v": "cv", "a": "ca", "p": "cp", "g": "cg"}
+    cnt, known, waited, hist = {}, {q: {} for q in Q}, {}, []
+    ADD, MUL, SUB = AluOpType.add, AluOpType.mult, AluOpType.subtract
+    COPY = ActivationFunctionType.Copy
+
+    def rg(name, c0=0, c1=None, step=1, p0=0, p1=128):
+        return (name, p0, p1, c0, SCRATCH[name][1][1] if c1 is None else c1, step)
+
+    def ap(x):
+        n, p0, p1, c0, c1, st = x
+        return T[n][p0:p1, c0:c1] if st == 1 else T[n][p0:p1, c0:c1:st]
+
+    def meet(x, y):
+        if x[0] != y[0]:
+            return False
+        if x[0].startswith("ps"):
+            return True
+        if x[2] <= y[1] or y[2] <= x[1] or x[4] <= y[3] or y[4] <= x[3]:
+            return False
+        if x[5] == 1 and y[5] == 1:
+            return True
+        return bool(set(range(x[3], x[4], x[5])) & set(range(y[3], y[4], y[5])))
+
+    def wait(q, ev):
+        sem, n, clock = ev
+        if known[q].get(sem, 0) >= n:
+            return
+        Q[q].wait_ge(T.sem[sem], n)
+        waited[sem] = max(waited.get(sem, 0), n)
+        for k, v in clock.items():
+            known[q][k] = max(known[q].get(k, 0), v)
+        known[q][sem] = n
+
+    def order(q, reads, writes):
+        need = {}
+        for x, wr, ev, eq in hist:
+            hit = any(meet(x, y) for y in writes)
+            if not hit and (wr or (x[0].startswith("ps") and eq != q)):
+                hit = any(meet(x, y) for y in reads)
+            if hit and (ev[0] not in need or need[ev[0]][1] < ev[1]):
+                need[ev[0]] = ev
+        evs = list(need.values())
+        for ev in evs:
+            if not any(o is not ev and o[2].get(ev[0], 0) >= ev[1] for o in evs):
+                wait(q, ev)
+
+    def note(q, ev, reads, writes):
+        for x in reads:
+            hist.append((x, False, ev, q))
+        for x in writes:
+            hist.append((x, True, ev, q))
+
+    def op(q, fn, reads, writes):
+        order(q, reads, writes)
+        sem = CS[q]
+        fn().then_inc(T.sem[sem], 1)
+        cnt[sem] = cnt.get(sem, 0) + 1
+        note(q, (sem, cnt[sem], dict(known[q])), reads, writes)
+
+    def dma(q, sem, out, in_, reads, writes):
+        order(q, reads, writes)
+        Q[q].dma_start(out, in_).then_inc(T.sem[sem], 16)
+        cnt[sem] = cnt.get(sem, 0) + 16
+        note(q, (sem, cnt[sem], dict(known[q])), reads, writes)
+
+    def lands(sem, n, writes):
+        cnt[sem] = n
+        note("far", (sem, n, {}), [], writes)
+
+    def copy(q, out, in_, scale=None):
+        if q == "a":
+            if scale is None:
+                op(q, lambda: g.scalar.activation(ap(out), ap(in_), COPY), [in_], [out])
+            else:
+                op(q, lambda: g.scalar.activation(ap(out), ap(in_), COPY, scale=scale), [in_], [out])
+        else:
+            op(q, lambda: g.vector.tensor_copy(ap(out), ap(in_)), [in_], [out])
+
+    def gather(q, out, win, off, scale=None):
+        if q == "a":
+            if scale is None:
+                op(q, lambda: g.scalar.activation(ap(out), ap(win).indirect(ap(off)), COPY), [win, off], [out])
+            else:
+                op(q, lambda: g.scalar.activation(ap(out), ap(win).indirect(ap(off)), COPY, scale=scale), [win, off], [out])
+        elif scale is None:
+            op(q, lambda: g.vector.tensor_copy(ap(out), ap(win).indirect(ap(off))), [win, off], [out])
+        else:
+            op(q, lambda: g.vector.tensor_scalar(ap(out), ap(win).indirect(ap(off)), scale, None, MUL), [win, off], [out])
+
+    def split(out, win, offn, o):
+        gather("v", rg(out, 0, H), rg(win), rg(offn, o, o + 16))
+        gather("a", rg(out, H, C), rg(win), rg(offn, o + 16, o + 32))
+
+    def tt(out, a, b, alu, off=None):
+        if off is None:
+            op("v", lambda: g.vector.tensor_tensor(ap(out), ap(a), ap(b), alu), [a, b], [out])
+        else:
+            op("v", lambda: g.vector.tensor_tensor(ap(out), ap(a).indirect(ap(off)), ap(b), alu), [a, b, off], [out])
+
+    def ts(out, a, s1, op0, s2=None, op1=None):
+        col = [s1] if isinstance(s1, tuple) else []
+        v1 = ap(s1) if col else s1
+        if op1 is None:
+            op("v", lambda: g.vector.tensor_scalar(ap(out), ap(a), v1, None, op0), [a] + col, [out])
+        else:
+            op("v", lambda: g.vector.tensor_scalar(ap(out), ap(a), v1, s2, op0, op1), [a] + col, [out])
+
+    def tr(out, in_):
+        op("v", lambda: g.vector.transpose(ap(out), ap(in_)), [in_], [out])
+
+    def scan(out, data):
+        op("v", lambda: g.vector.tensor_tensor_scan(ap(out), ap(rg("rst")), ap(data), 0.0, MUL, ADD), [rg("rst"), data], [out])
+
+    def quant(q, s, tile, a, b):
+        o1, o2, i = rg(q, a, b), rg(s, a, b), rg(tile, 4 * a, 4 * b)
+        op("v", lambda: g.vector.quantize_mx(ap(o1), ap(o2), ap(i)), [i], [o1, o2])
+
+    def mm(bank, wq, ws, w0, xq, xs, a, b):
+        o, i = rg("ps%d" % bank, 0, b - a), [rg(wq, w0, w0 + 128), rg(ws, w0, w0 + 128), rg(xq, a, b), rg(xs, a, b)]
+        op("p", lambda: g.tensor.matmul_mx(ap(o), ap(i[0]), ap(i[1]), ap(i[2]), ap(i[3]), True, True), i, [o])
+
+    def pick_codes(out, win, off):
+        op("v", lambda: g.vector.tensor_copy(ap(out).bitcast(dt.uint32), ap(win).bitcast(dt.uint32).indirect(ap(off))), [win, off], [out])
+
+    def iota(out, pattern, base, cm, flt):
+        if flt:
+            op("g", lambda: g.iota(ap(out), pattern, base, cm, allow_small_or_imprecise_dtypes=True), [], [out])
+        else:
+            op("g", lambda: g.iota(ap(out), pattern, base, cm), [], [out])
+
+    def wrap(out, win, off, m, s):
+        tt(rg(m), win, rg("mask"), MUL, off)
+        scan(rg(s), rg(m))
+        if out is not None:
+            copy("v", out, rg(s, 15, C, 16))
+
+    def list_dsts(k):
+        return [] if k == N - 1 else [d for d in range(N) if d > k or (d == 0 and k > 0)]
+
+    def full(src, dst):
+        return topo.mask(cores[src], cores[dst]), len(topo.engines(cores[src], cores[dst]))
+
+    def cut_of(k, t):
+        return CFG["cut"][t] if k == N - 1 else H
+
+    nxt, prv = (r + 1) % N, (r - 1) % N
+
+    dma("a", "ld1", ap(rg("ub")), T.u[:, :], [], [rg("ub")])
+    dma("s", "ld2", ap(rg("x0", 0, 4 * H)), T.x[:, 0:4 * H], [], [rg("x0", 0, 4 * H)])
+    dma("s", "ld3", ap(rg("x0", 4 * H, 4 * C)), T.x[:, 4 * H:4 * C], [], [rg("x0", 4 * H, 4 * C)])
+    dma("s", "ld0", ap(rg("pri")), T.pr[:, :], [], [rg("pri")])
+    order("s", [rg("x0")], [])
+    dma("s", "ld4", ap(rg("vq")).bitcast(dt.uint8), T.vc[:, :], [], [rg("vq")])
+    dma("s", "ld5", ap(rg("vp")), T.vs[:, :], [], [rg("vp")])
+    dma("s", "ld6", ap(rg("wq")).bitcast(dt.uint8), T.wc[:, :], [], [rg("wq")])
+    dma("s", "ld7", ap(rg("wp")), T.ws[:, :], [], [rg("wp")])
+    dma("s", "ld8", ap(rg("ab")), T.a[:, :], [], [rg("ab")])
+
+    iota(rg("pcol"), [[0, 2]], 0, 1, False)
+    iota(rg("k16"), [[16, 32]], 0, 0, True)
+    iota(rg("jm"), [[0, 32], [1, 16]], 0, 0, True)
+    iota(rg("row"), [[1, C]], 0, 0, True)
+    op("v", lambda: g.vector.memset(ap(rg("rst")), 1.0), [], [rg("rst")])
+    op("v", lambda: g.vector.memset(ap(rg("rst", 0, C, 16)), 0.0), [], [rg("rst", 0, C, 16)])
+    ts(rg("pand"), rg("pcol"), 15, AluOpType.bitwise_and)
+    copy("v", rg("uoff"), rg("k16", 0, 8))
+    copy("v", rg("pm"), rg("pand"))
+    ts(rg("jw"), rg("k16"), rg("pm", 0, 1), ADD)
+    for k in range(2):
+        tr(rg("asm", 32 * k, 32 * k + 32), rg("jw"))
+    copy("v", rg("o4", 0, 32, 1, 0, 64), rg("jw", 0, 32, 1, 0, 64))
+    ts(rg("mbig"), rg("jm"), rg("pm", 0, 1), AluOpType.not_equal, BIG, MUL)
+    quant("uq", "us", "ub", 0, 128)
+    pick_codes(rg("uq2"), rg("uq"), rg("uoff"))
+    gather("a", rg("us2"), rg("us"), rg("uoff"))
+    op("a", lambda: g.scalar.activation(ap(rg("mask")), ap(rg("mbig")), ActivationFunctionType.Identity, bias=1.0, scale=-1.0 / BIG),
+       [rg("mbig")], [rg("mask")])
+    for h in range(2):
+        quant("xq0", "xs0", "x0", h * H, h * H + H)
+
+    for t in range(R):
+        last = t == R - 1
+        X, xq, xs = "x%d" % t, "xq%d" % t, "xs%d" % t
+        X2, xq2, xs2 = "x%d" % (t + 1), "xq%d" % (t + 1), "xs%d" % (t + 1)
+        off, lr, bw = "off%d" % t, "lr%d" % t, "bw%d" % t
+        Y, yq, yp, zq, zp, kq, kp = ["%s%d" % (n, t) for n in ("yt", "yq", "yp", "zq", "zp", "kq", "kp")]
+        av, mx = "av%d" % t, "mx%d" % t
+
+        def L(k):
+            return rg(lr, 32 * k, 32 * k + 32)
+
+        for k in range(N):
+            if r in list_dsts(k):
+                lands("lst%d_%d" % (t, k), len(_list_masks(topo, cores[k], [cores[d] for d in list_dsts(k)])[core]), [L(k)])
+        ne, cut = full(prv, r)[1], cut_of(prv, t)
+        if CFG["calls"][prv] == 4:
+            lands("dat%d_0" % t, 2 * ne, [rg(zq, 0, cut), rg(zp, 0, cut)])
+            lands("dat%d_1" % t, 2 * ne, [rg(zq, cut, C), rg(zp, cut, C)])
+        elif CFG["calls"][prv] == 3:
+            lands("dat%d_0" % t, ne, [rg(zq, 0, cut)])
+            lands("dat%d_1" % t, 2 * ne, [rg(zq, cut, C), rg(zp)])
+        else:
+            lands("dat%d_1" % t, 2 * ne, [rg(zq), rg(zp)])
+
+        for h in range(2):
+            mm(4 + h, "uq2", "us2", 0, xq, xs, h * H, h * H + H)
+            mm(h, "uq2", "us2", 0, xq, xs, h * H, h * H + H)
+        for h in range(2):
+            copy("a", rg("sv", h * H, h * H + H), rg("ps%d" % h, 0, H))
+            tt(rg("thr", h * H, h * H + H), rg("mbig", h * H, h * H + H), rg("ps%d" % (4 + h), 0, H), SUB)
+        if t == 0:
+            copy("v", rg("pro"), rg("pri"))
+            tt(rg("dd"), rg("pri"), rg("jw"), SUB)
+        tt(rg("vb"), rg("sv"), rg("thr"), AluOpType.is_gt, rg("pro"))
+        scan(rg("wb"), rg("vb"))
+        tt(rg("t1"), rg("wb", 15, C, 16), rg("dd"), MUL)
+        tt(rg("cw"), rg("t1"), rg("jw"), ADD)
+        copy("v", rg("o0"), rg("cw"))
+        tr(rg("asm", 64, 96), rg("cw"))
+        gather("a", rg("ta"), rg("row"), rg("o0"))
+        for a in range(3):
+            copy("v", rg("asm", 32, 64, 1, 32 * a + 32, 32 * a + 64), rg("asm", 64, 96, 1, 32 * a, 32 * a + 32))
+        copy("v", rg("asm", 0, 32, 1, 64, 128), rg("asm", 64, 96, 1, 0, 64))
+        tr(rg("bt", 0, 64), rg("asm", 16, 80))
+        tr(rg("bt", 64, 96), rg("asm", 32, 64))
+        copy("v", rg("ou"), rg("bt"))
+
+        split("tb", "ta", "ou", 32)
+        split("ta", "tb", "ou", 64)
+        gather("a", rg("tb"), rg("ta"), rg("ou", 0, 32))
+        wrap(None, rg("ta"), rg("ou", 0, 32), "tm4", "ts4")
+        copy("v", rg("o4", 0, 32, 1, 64, 128), rg("ts4", 15, C, 16, 0, 64))
+        if last:
+            gather("a", rg("t7"), rg("tb"), rg("o4"))
+        wrap(None, rg("tb"), rg("o4"), "tm", "ts")
+
+        def offs(k):
+            ts(rg(off, 32 * k, 32 * k + 32), rg("ts", 15, C, 16), 4.0, MUL, float(k), ADD)
+
+        dsts = list_dsts(r)
+        if dsts:
+            offs(0)
+            tr(rg("sa", 0, 32, 1, 96, 128), rg("ts", 15, C, 16, 96, 128))
+            offs(1)
+            copy("v", rg("sa", 0, 16, 1, 96, 128), rg("sa", 16, 32, 1, 96, 128))
+            offs(2)
+            tr(rg("sc", 0, 32, 1, 96, 128), rg("sa", 0, 32, 1, 96, 128))
+            offs(3)
+            for q in range(4):
+                copy("v", rg(lr, 32 * r, 32 * r + 32, 1, 32 * q, 32 * q + 32), rg("sc", 0, 32, 1, 96, 128))
+            em = _list_masks(topo, core, [cores[d] for d in dsts])
+            order("g", [L(r)], [])
+            trs = []
+            for d in dsts:
+                rid, pid, _ = topo.addr(cores[d])
+                trs.append(RemoteDMATransfer(dst_ids=[DstId(rid=rid, pnc=pid)], dma_engine_mask=sum(1 << e for e in em[cores[d]]),
+                                             remote_sem=T.sem["lst%d_%d" % (t, r)], src=ap(L(r)), dst=ap(L(r))))
+                cnt["sent"] = cnt.get("sent", 0) + len(em[cores[d]])
+            g.remote_dma_fused(trs, local_sem=T.sem.sent)
+        else:
+            for k in range(4):
+                offs(k)
+
+        rid, pid, _ = topo.addr(cores[nxt])
+        msk, ne = full(r, nxt)
+        calls, cut = CFG["calls"][r], cut_of(r, t)
+
+        def send(out, in_, h):
+            g.remote_dma(out, in_, T.sem["dat%d_%d" % (t, h)], T.sem.sent, pid, rid, msk)
+            cnt["sent"] = cnt.get("sent", 0) + ne
+
+        def ypart(q, k, a, b):
+            gather(q, rg(Y, 4 * a + k, 4 * b, 4), rg(X), rg(off, 32 * k + a // 16, 32 * k + b // 16))
+
+        for h in range(2):
+            a, b = (0, cut) if h == 0 else (cut, C)
+            mid = (a + b) // 2
+            ypart("a", 0, a, b)
+            ypart("a", 1, a, b)
+            if h == 0:
+                ypart("a" if dsts else "v", 2, a, b)
+                ypart("v", 3, a, b)
+            else:
+                ypart("a", 2, a, mid)
+                ypart("v", 3, a, b)
+                ypart("v", 2, mid, b)
+            quant(yq, yp, Y, a, b)
+            if calls == 2:
+                if h == 0:
+                    continue
+                a = 0
+            order("g", [rg(yq, a, b)], [])
+            send(ap(rg(zq, a, b)).bitcast(dt.uint8), ap(rg(yq, a, b)).bitcast(dt.uint8), h)
+            if calls == 4:
+                send(ap(rg(zp, a, b)), ap(rg(yp, a, b)), h)
+            elif h == 1:
+                send(ap(rg(zp)), ap(rg(yp)), h)
+
+        def vcopy(h):
+            for b in range(4):
+                copy("a", rg(av, C * b + h * H, C * b + h * H + H), rg("ps%d" % b, h * H, h * H + H))
+
+        def pick(iq, ip, lst, a=0, b=C):
+            o = rg(lst[0], lst[3] + a // 16, lst[3] + b // 16)
+            pick_codes(rg(kq, a, b), rg(iq), o)
+            gather("a", rg(kp, a, b), rg(ip), o)
+
+        def vmax(b, h):
+            tt(rg(mx, C * b + h * H, C * b + h * H + H), rg("ps%d" % (4 + b), 0, H), rg(av, C * b + h * H, C * b + h * H + H), AluOpType.max)
+
+        def xcols(b, h):
+            return rg(X2, 4 * h * H + b, 4 * (h * H + H), 4)
+
+        def plain(b, h):
+            copy("a", xcols(b, h), rg(mx, C * b + h * H, C * b + h * H + H), SC)
+
+        def undo(q, b, h):
+            gather(q, xcols(b, h), rg(mx, C * b, C * b + C), rg(back[0], back[3] + 16 * h, back[3] + 16 * h + 16), SC)
+
+        back = None
+        if r == 0:
+            for b in range(4):
+                mm(b, "vq", "vp", 128 * b, yq, yp, 0, C)
+            vcopy(0)
+            if last:
+                dma("s", "outs", T.ol[:, :], T.t7[0:128:16, :], [rg("t7")], [])
+            if t == 0:
+                quant("aq", "asc", "ab", 0, 128)
+            split("la", "row", lr, 64)
+            split("lb", "la", lr, 32)
+            vcopy(1)
+            wrap(rg(bw), rg("lb"), L(0), "tm2", "ts2")
+            for h in range(2):
+                pick(zq, zp, rg(bw), h * H, h * H + H)
+            wq_, wp_ = kq, kp
+        else:
+            if t == 0:
+                quant("aq", "asc", "ab", 0, 128)
+            pick(yq, yp, L(r - 1))
+            if r == 3:
+                split("la", "row", lr, 32)
+            for b in range(4):
+                mm(b, "vq", "vp", 128 * b, kq, kp, 0, C)
+            wq_, wp_ = zq, zp
+            if r == 1:
+                if last:
+                    gather("v", rg("t8"), rg("t7"), L(0))
+                    dma("s", "outs", T.ol[:, :], T.t8[0:128:16, :], [rg("t8")], [])
+            elif r == 2:
+                back = L(0)
+                if last:
+                    gather("a", rg("t8"), rg("t7"), L(1))
+                    gather("v", rg("t9"), rg("t8"), L(0))
+                    dma("s", "outs", T.ol[:, :], T.t9[0:128:16, :], [rg("t9")], [])
+            else:
+                wrap(rg(bw), rg("la"), L(0), "tm2", "ts2")
+                back = rg(bw)
+            vcopy(0)
+            vcopy(1)
+
+        for b in range(4):
+            mm(4 + b, "wq", "wp", 128 * b, wq_, wp_, 0, H)
+        for b in range(4):
+            vmax(b, 0)
+            mm(4 + b, "wq", "wp", 128 * b, wq_, wp_, H, C)
+            if back is None:
+                plain(b, 0)
+        for b in range(4):
+            vmax(b, 1)
+            if back is None:
+                plain(b, 1)
+                if b == 1:
+                    quant(xq2, xs2, X2, 0, H)
+        if back is None:
+            quant(xq2, xs2, X2, H, C)
+        else:
+            for b, h in ((0, 0), (1, 0), (2, 0), (0, 1), (1, 1)):
+                undo("a", b, h)
+            undo("v", 3, 0)
+            undo("v", 3, 1)
+            quant(xq2, xs2, X2, 0, H)
+            undo("v", 2, 1)
+            quant(xq2, xs2, X2, H, C)
+
+    xq, xs = "xq%d" % R, "xs%d" % R
+    if r == N - 1:
+        gather("a", rg("t8"), rg("t7"), rg("lr%d" % (R - 1), 64, 96))
+    for h in range(2):
+        mm(4 * h, "aq", "asc", 0, xq, xs, h * H, h * H + H)
+        dma("s", "outs", T.oc[:, 4 * h * H:4 * (h * H + H)], ap(rg(xq, h * H, h * H + H)).bitcast(dt.uint8), [rg(xq, h * H, h * H + H)], [])
+    for k in range(4):
+        dma("s", "outs", T.osc[4 * k:4 * k + 4, :], T[xs][32 * k:32 * k + 4, :], [rg(xs)], [])
+    for h in range(2):
+        copy("a" if h == 0 and r < N - 1 else "v", rg("ysb", h * H, h * H + H), rg("ps%d" % (4 * h), 0, H))
+        dma("s" if r == N - 1 else "a", "outs", T.y[:, h * H:h * H + H], ap(rg("ysb", h * H, h * H + H)), [rg("ysb", h * H, h * H + H)], [])
+    if r == N - 1:
+        split("t9", "t8", "bw%d" % (R - 1), 0)
+        dma("a", "outs", T.ol[:, :], T.t9[0:128:16, :], [rg("t9")], [])
+
+    for sem in sorted(cnt, key=lambda k: k == "outs"):
+        if waited.get(sem, 0) < cnt[sem]:
+            g.wait_ge(T.sem[sem], cnt[sem])

@@ -8,7 +8,6 @@ SC = 0.03125
 BIG = 2.0 ** 96
 LT = "float16"
 X4 = "float8_e4m3fn_x4"
-CFG = {"calls": (4, 4, 4, 3), "cut": (128, 256)}
 
 
 def _scratch():
@@ -84,6 +83,7 @@ def rank_program(g, core, T, topo):
     cnt, known, waited, hist = {}, {q: {} for q in Q}, {}, []
     ADD, MUL, SUB = AluOpType.add, AluOpType.mult, AluOpType.subtract
     COPY = ActivationFunctionType.Copy
+    HALVES = ((0, H), (H, C))
 
     def rg(name, c0=0, c1=None, step=1, p0=0, p1=128):
         return (name, p0, p1, c0, SCRATCH[name][1][1] if c1 is None else c1, step)
@@ -191,7 +191,8 @@ def rank_program(g, core, T, topo):
         op("v", lambda: g.vector.transpose(ap(out), ap(in_)), [in_], [out])
 
     def scan(out, data):
-        op("v", lambda: g.vector.tensor_tensor_scan(ap(out), ap(rg("rst")), ap(data), 0.0, MUL, ADD), [rg("rst"), data], [out])
+        rst = rg("rst", data[3], data[4])
+        op("v", lambda: g.vector.tensor_tensor_scan(ap(out), ap(rst), ap(data), 0.0, MUL, ADD), [rst, data], [out])
 
     def quant(q, s, tile, a, b):
         o1, o2, i = rg(q, a, b), rg(s, a, b), rg(tile, 4 * a, 4 * b)
@@ -210,20 +211,20 @@ def rank_program(g, core, T, topo):
         else:
             op("g", lambda: g.iota(ap(out), pattern, base, cm), [], [out])
 
-    def wrap(out, win, off, m, s):
-        tt(rg(m), win, rg("mask"), MUL, off)
-        scan(rg(s), rg(m))
+    def wrap(out, win, off, m, s, other="mask", alu=MUL):
+        for a, b in HALVES:
+            tt(rg(m, a, b), win, rg(other, a, b), alu, rg(off[0], off[3] + a // 16, off[3] + b // 16))
+        for a, b in HALVES:
+            scan(rg(s, a, b), rg(m, a, b))
         if out is not None:
-            copy("v", out, rg(s, 15, C, 16))
+            for a, b in HALVES:
+                copy("v", rg(out[0], a // 16, b // 16, 1, out[1], out[2]), rg(s, a + 15, b, 16, 0, out[2] - out[1]))
 
     def list_dsts(k):
         return [] if k == N - 1 else [d for d in range(N) if d > k or (d == 0 and k > 0)]
 
     def full(src, dst):
         return topo.mask(cores[src], cores[dst]), len(topo.engines(cores[src], cores[dst]))
-
-    def cut_of(k, t):
-        return CFG["cut"][t] if k == N - 1 else H
 
     nxt, prv = (r + 1) % N, (r - 1) % N
 
@@ -257,8 +258,8 @@ def rank_program(g, core, T, topo):
     gather("a", rg("us2"), rg("us"), rg("uoff"))
     op("a", lambda: g.scalar.activation(ap(rg("mask")), ap(rg("mbig")), ActivationFunctionType.Identity, bias=1.0, scale=-1.0 / BIG),
        [rg("mbig")], [rg("mask")])
-    for h in range(2):
-        quant("xq0", "xs0", "x0", h * H, h * H + H)
+    for a, b in HALVES:
+        quant("xq0", "xs0", "x0", a, b)
 
     for t in range(R):
         last = t == R - 1
@@ -274,15 +275,13 @@ def rank_program(g, core, T, topo):
         for k in range(N):
             if r in list_dsts(k):
                 lands("lst%d_%d" % (t, k), len(_list_masks(topo, cores[k], [cores[d] for d in list_dsts(k)])[core]), [L(k)])
-        ne, cut = full(prv, r)[1], cut_of(prv, t)
-        if CFG["calls"][prv] == 4:
-            lands("dat%d_0" % t, 2 * ne, [rg(zq, 0, cut), rg(zp, 0, cut)])
-            lands("dat%d_1" % t, 2 * ne, [rg(zq, cut, C), rg(zp, cut, C)])
-        elif CFG["calls"][prv] == 3:
-            lands("dat%d_0" % t, ne, [rg(zq, 0, cut)])
-            lands("dat%d_1" % t, 2 * ne, [rg(zq, cut, C), rg(zp)])
+        ne = full(prv, r)[1]
+        if r > 0:
+            lands("dat%d_0" % t, 2 * ne, [rg(zq, 0, H), rg(zp, 0, H)])
+            lands("dat%d_1" % t, 2 * ne, [rg(zq, H, C), rg(zp, H, C)])
         else:
-            lands("dat%d_1" % t, 2 * ne, [rg(zq), rg(zp)])
+            lands("dat%d_0" % t, ne, [rg(zq, 0, H)])
+            lands("dat%d_1" % t, 2 * ne, [rg(zq, H, C), rg(zp)])
 
         for h in range(2):
             mm(4 + h, "uq2", "us2", 0, xq, xs, h * H, h * H + H)
@@ -293,8 +292,7 @@ def rank_program(g, core, T, topo):
         if t == 0:
             copy("v", rg("pro"), rg("pri"))
             tt(rg("dd"), rg("pri"), rg("jw"), SUB)
-        tt(rg("vb"), rg("sv"), rg("thr"), AluOpType.is_gt, rg("pro"))
-        scan(rg("wb"), rg("vb"))
+        wrap(None, rg("sv"), rg("pro"), "vb", "wb", "thr", AluOpType.is_gt)
         tt(rg("t1"), rg("wb", 15, C, 16), rg("dd"), MUL)
         tt(rg("cw"), rg("t1"), rg("jw"), ADD)
         copy("v", rg("o0"), rg("cw"))
@@ -310,42 +308,48 @@ def rank_program(g, core, T, topo):
         split("tb", "ta", "ou", 32)
         split("ta", "tb", "ou", 64)
         gather("a", rg("tb"), rg("ta"), rg("ou", 0, 32))
-        wrap(None, rg("ta"), rg("ou", 0, 32), "tm4", "ts4")
-        copy("v", rg("o4", 0, 32, 1, 64, 128), rg("ts4", 15, C, 16, 0, 64))
+        wrap(rg("o4", 0, 32, 1, 64, 128), rg("ta"), rg("ou", 0, 32), "tm4", "ts4")
         if last:
             gather("a", rg("t7"), rg("tb"), rg("o4"))
         wrap(None, rg("tb"), rg("o4"), "tm", "ts")
 
-        def offs(k):
-            ts(rg(off, 32 * k, 32 * k + 32), rg("ts", 15, C, 16), 4.0, MUL, float(k), ADD)
+        def offs(k, a=0, b=C):
+            ts(rg(off, 32 * k + a // 16, 32 * k + b // 16), rg("ts", a + 15, b, 16), 4.0, MUL, float(k), ADD)
 
         dsts = list_dsts(r)
+        offs(0, 0, H)
+        offs(1, 0, H)
         if dsts:
-            offs(0)
             tr(rg("sa", 0, 32, 1, 96, 128), rg("ts", 15, C, 16, 96, 128))
-            offs(1)
-            copy("v", rg("sa", 0, 16, 1, 96, 128), rg("sa", 16, 32, 1, 96, 128))
             offs(2)
-            tr(rg("sc", 0, 32, 1, 96, 128), rg("sa", 0, 32, 1, 96, 128))
+            offs(0, H, C)
+            copy("v", rg("sa", 0, 16, 1, 96, 128), rg("sa", 16, 32, 1, 96, 128))
             offs(3)
+            offs(1, H, C)
+            tr(rg("sc", 0, 32, 1, 96, 128), rg("sa", 0, 32, 1, 96, 128))
             for q in range(4):
                 copy("v", rg(lr, 32 * r, 32 * r + 32, 1, 32 * q, 32 * q + 32), rg("sc", 0, 32, 1, 96, 128))
             em = _list_masks(topo, core, [cores[d] for d in dsts])
             order("g", [L(r)], [])
-            trs = []
+            trs, late = [], []
             for d in dsts:
                 rid, pid, _ = topo.addr(cores[d])
-                trs.append(RemoteDMATransfer(dst_ids=[DstId(rid=rid, pnc=pid)], dma_engine_mask=sum(1 << e for e in em[cores[d]]),
-                                             remote_sem=T.sem["lst%d_%d" % (t, r)], src=ap(L(r)), dst=ap(L(r))))
+                x = RemoteDMATransfer(dst_ids=[DstId(rid=rid, pnc=pid)], dma_engine_mask=sum(1 << e for e in em[cores[d]]),
+                                      remote_sem=T.sem["lst%d_%d" % (t, r)], src=ap(L(r)), dst=ap(L(r)))
+                own = set(em[cores[d]]) <= set(topo.engines(core, cores[nxt]))
+                (trs if own or t > 0 else late).append(x)
                 cnt["sent"] = cnt.get("sent", 0) + len(em[cores[d]])
             g.remote_dma_fused(trs, local_sem=T.sem.sent)
+            if late:
+                g.remote_dma_fused(late, local_sem=T.sem.sent)
         else:
-            for k in range(4):
-                offs(k)
+            offs(2)
+            offs(3)
+            offs(0, H, C)
+            offs(1, H, C)
 
         rid, pid, _ = topo.addr(cores[nxt])
         msk, ne = full(r, nxt)
-        calls, cut = CFG["calls"][r], cut_of(r, t)
 
         def send(out, in_, h):
             g.remote_dma(out, in_, T.sem["dat%d_%d" % (t, h)], T.sem.sent, pid, rid, msk)
@@ -354,8 +358,7 @@ def rank_program(g, core, T, topo):
         def ypart(q, k, a, b):
             gather(q, rg(Y, 4 * a + k, 4 * b, 4), rg(X), rg(off, 32 * k + a // 16, 32 * k + b // 16))
 
-        for h in range(2):
-            a, b = (0, cut) if h == 0 else (cut, C)
+        for h, (a, b) in enumerate(HALVES):
             mid = (a + b) // 2
             ypart("a", 0, a, b)
             ypart("a", 1, a, b)
@@ -367,22 +370,14 @@ def rank_program(g, core, T, topo):
                 ypart("v", 3, a, b)
                 ypart("v", 2, mid, b)
             quant(yq, yp, Y, a, b)
-            if calls == 2:
-                if h == 0:
-                    continue
-                a = 0
             order("g", [rg(yq, a, b)], [])
             send(ap(rg(zq, a, b)).bitcast(dt.uint8), ap(rg(yq, a, b)).bitcast(dt.uint8), h)
-            if calls == 4:
+            if nxt > 0:
                 send(ap(rg(zp, a, b)), ap(rg(yp, a, b)), h)
             elif h == 1:
                 send(ap(rg(zp)), ap(rg(yp)), h)
 
-        def vcopy(h):
-            for b in range(4):
-                copy("a", rg(av, C * b + h * H, C * b + h * H + H), rg("ps%d" % b, h * H, h * H + H))
-
-        def pick(iq, ip, lst, a=0, b=C):
+        def pick(iq, ip, lst, a, b):
             o = rg(lst[0], lst[3] + a // 16, lst[3] + b // 16)
             pick_codes(rg(kq, a, b), rg(iq), o)
             gather("a", rg(kp, a, b), rg(ip), o)
@@ -399,30 +394,44 @@ def rank_program(g, core, T, topo):
         def undo(q, b, h):
             gather(q, xcols(b, h), rg(mx, C * b, C * b + C), rg(back[0], back[3] + 16 * h, back[3] + 16 * h + 16), SC)
 
+        todo = [(b, h) for h in range(2) for b in range(4)]
+
+        def vcopy(n):
+            while len(todo) > 8 - n:
+                b, h = todo.pop(0)
+                src = rg("ps%d" % b, h * H, h * H + H) if r == 0 else rg("ps%d" % (b + 4 - 4 * h), 0, H)
+                copy("a", rg(av, C * b + h * H, C * b + h * H + H), src)
+
         back = None
         if r == 0:
             for b in range(4):
                 mm(b, "vq", "vp", 128 * b, yq, yp, 0, C)
-            vcopy(0)
             if last:
                 dma("s", "outs", T.ol[:, :], T.t7[0:128:16, :], [rg("t7")], [])
-            if t == 0:
+            else:
+                vcopy(2)
                 quant("aq", "asc", "ab", 0, 128)
             split("la", "row", lr, 64)
             split("lb", "la", lr, 32)
-            vcopy(1)
+            vcopy(6)
             wrap(rg(bw), rg("lb"), L(0), "tm2", "ts2")
-            for h in range(2):
-                pick(zq, zp, rg(bw), h * H, h * H + H)
+            for a, b in HALVES:
+                pick(zq, zp, rg(bw), a, b)
+            vcopy(8)
             wq_, wp_ = kq, kp
         else:
             if t == 0:
                 quant("aq", "asc", "ab", 0, 128)
-            pick(yq, yp, L(r - 1))
-            if r == 3:
+            if r == 3 and last:
+                split("la", "row", lr, 32)
+            pick(yq, yp, L(r - 1), 0, H)
+            for b in range(4):
+                mm(4 + b, "vq", "vp", 128 * b, kq, kp, 0, H)
+            pick(yq, yp, L(r - 1), H, C)
+            if r == 3 and not last:
                 split("la", "row", lr, 32)
             for b in range(4):
-                mm(b, "vq", "vp", 128 * b, kq, kp, 0, C)
+                mm(b, "vq", "vp", 128 * b, kq, kp, H, C)
             wq_, wp_ = zq, zp
             if r == 1:
                 if last:
@@ -431,14 +440,11 @@ def rank_program(g, core, T, topo):
             elif r == 2:
                 back = L(0)
                 if last:
-                    gather("a", rg("t8"), rg("t7"), L(1))
-                    gather("v", rg("t9"), rg("t8"), L(0))
-                    dma("s", "outs", T.ol[:, :], T.t9[0:128:16, :], [rg("t9")], [])
+                    gather("v", rg("t8"), rg("t7"), L(1))
             else:
                 wrap(rg(bw), rg("la"), L(0), "tm2", "ts2")
                 back = rg(bw)
-            vcopy(0)
-            vcopy(1)
+            vcopy(8)
 
         for b in range(4):
             mm(4 + b, "wq", "wp", 128 * b, wq_, wp_, 0, H)
@@ -451,9 +457,8 @@ def rank_program(g, core, T, topo):
             vmax(b, 1)
             if back is None:
                 plain(b, 1)
-                if b == 1:
-                    quant(xq2, xs2, X2, 0, H)
         if back is None:
+            quant(xq2, xs2, X2, 0, H)
             quant(xq2, xs2, X2, H, C)
         else:
             for b, h in ((0, 0), (1, 0), (2, 0), (0, 1), (1, 1)):
@@ -467,14 +472,17 @@ def rank_program(g, core, T, topo):
     xq, xs = "xq%d" % R, "xs%d" % R
     if r == N - 1:
         gather("a", rg("t8"), rg("t7"), rg("lr%d" % (R - 1), 64, 96))
+    if r == 2:
+        gather("a", rg("t9"), rg("t8"), rg("lr%d" % (R - 1), 0, 32))
+        dma("a", "outs", T.ol[:, :], T.t9[0:128:16, :], [rg("t9")], [])
     for h in range(2):
         mm(4 * h, "aq", "asc", 0, xq, xs, h * H, h * H + H)
         dma("s", "outs", T.oc[:, 4 * h * H:4 * (h * H + H)], ap(rg(xq, h * H, h * H + H)).bitcast(dt.uint8), [rg(xq, h * H, h * H + H)], [])
     for k in range(4):
         dma("s", "outs", T.osc[4 * k:4 * k + 4, :], T[xs][32 * k:32 * k + 4, :], [rg(xs)], [])
     for h in range(2):
-        copy("a" if h == 0 and r < N - 1 else "v", rg("ysb", h * H, h * H + H), rg("ps%d" % (4 * h), 0, H))
-        dma("s" if r == N - 1 else "a", "outs", T.y[:, h * H:h * H + H], ap(rg("ysb", h * H, h * H + H)), [rg("ysb", h * H, h * H + H)], [])
+        copy("a" if h == 0 and r < 2 else "v", rg("ysb", h * H, h * H + H), rg("ps%d" % (4 * h), 0, H))
+        dma("s" if r >= 2 else "a", "outs", T.y[:, h * H:h * H + H], ap(rg("ysb", h * H, h * H + H)), [rg("ysb", h * H, h * H + H)], [])
     if r == N - 1:
         split("t9", "t8", "bw%d" % (R - 1), 0)
         dma("a", "outs", T.ol[:, :], T.t9[0:128:16, :], [rg("t9")], [])

@@ -5,9 +5,54 @@ C = 512
 R = 2
 H = C // 2
 SC = 0.03125
-BIG = 2.0 ** 96
-LT = "float16"
+MID = 256.0
+UP, DOWN = 4096.0, -1024.0
 X4 = "float8_e4m3fn_x4"
+
+PAR = {
+    "xcut": [[(0, 256, 384, 512)] * 3] * 4,
+    "ycut": [(0, 256, 512)] * 4,
+    "whole": [False, False, False, True],
+    "lists": [[[1, 2, 3]], [[2, 3, 0]], [[3, 0]], []],
+    "kcut": (0, 256, 512),
+    "pcut": (0, 256, 512),
+    "fcut": (0, 256, 384, 512),
+    "vcut": (0, 256, 512),
+    "wcut": (0, 128, 320, 512),
+    "bcut": (0, 128, 320, 512),
+    "yshare": 18,
+}
+
+ORDER = {
+    0: {
+        "v": "pi2 pi0 pi1 pf jw fx0 ka16 uoff fx1 id0 qu kb16 puc o4i qx0 wz qx1 e0 kk16 fx3 qx2 dd pro fd jw2 vb0.0 vb1.0 wb0.0 wb1.0 id1 cw.0 tn0.0 o0.0 tn1.0 tn2.0 tm.0 to.0 b2.0 b1.0 b3.0 ou1.0 ou2.0 g20.0 g30.0 g40.0 g42.0 s10.0 s11.0 s12.0 o40.0 o41.0 o42.0 g50.0 g52.0 s40.0 s41.0 s42.0 la.0 of2.0 lb.0 of0.0 lc3.0 lc2.0 of3.0 lr1.0 lr0.0 of1.0 qa y11.0 y10.0 qy0.0 qy1.0 av02.0 av10.0 La0.0 Lb1.0 Lc2.0 Lc0.0 s21.0 s20.0 s22.0 bw1.0 bw0.0 bw2.0 pk0c.0 pk1c.0 mx00.0 mx02.0 mx03.0 mx01.0 mx13.0 mx12.0 mx10.0 mx11.0 x10.0 qn0.0 x20.0 qn1.0 qn2.0 nv0.1 sv1.1 vb0.1 vb1.1 wb0.1 wb1.1 cw.1 tn0.1 o0.1 tm.1 tn2.1 tn1.1 to.1 b1.1 b3.1 b2.1 ou1.1 ou2.1 g20.1 g30.1 g42.1 s10.1 s12.1 s11.1 o40.1 o42.1 o41.1 g52.1 s40.1 s42.1 s41.1 la.1 of3.1 of2.1 lb.1 of1.1 of0.1 lc3.1 lc2.1 y00.1 lr1.1 lr0.1 y11.1 y13.1 qy0.1 La0.1 qy1.1 Lb0.1 av03.1 Lc1.1 av02.1 s21.1 s20.1 s22.1 bw1.1 bw0.1 bw2.1 pk0c.1 pk1c.1 mx00.1 mx02.1 mx03.1 mx01.1 mx13.1 mx10.1 mx11.1 mx12.1 qn0.1 x10.1 qn2.1 qn1.1 ys0",
+        "a": "lu pg fx2 pup sv0.0 nv0.0 sv1.0 sv2.0 nv1.0 nv2.0 g10.0 g21.0 g31.0 g41.0 g51.0 y12.0 y02.0 y13.0 y03.0 y01.0 y00.0 av01.0 La1.0 Lb0.0 Lc1.0 av03.0 av00.0 pk0p.0 av11.0 pk1p.0 av13.0 av12.0 x01.0 x00.0 x11.0 x21.0 sv0.1 sv2.1 nv1.1 nv2.1 g10.1 g21.1 g31.1 g40.1 g41.1 g50.1 g51.1 y03.1 y02.1 y01.1 y12.1 y10.1 La1.1 Lb1.1 av00.1 Lc0.1 Lc2.1 av13.1 av01.1 pk0p.1 av10.1 pk1p.1 ol av11.1 av12.1 x00.1 x01.1 x21.1 x20.1 x11.1 ys2 dy0 dy2 ys1 ds1",
+        "p": "ms0.0 mt0.0 ms1.0 ms2.0 mt1.0 mt2.0 mv02.0 mv10.0 mv01.0 mv00.0 mv03.0 mv11.0 mv13.0 mv12.0 mw00.0 mw02.0 mw03.0 mw01.0 mw10.0 mw13.0 mw12.0 mw11.0 ms0.1 mt0.1 ms1.1 ms2.1 mt1.1 mt2.1 mv02.1 mv00.1 mv03.1 mv11.1 mv13.1 mv01.1 mv12.1 mv10.1 mw00.1 mw02.1 mw01.1 mw03.1 mw10.1 mw13.1 mw11.1 mw12.1 my0 my2 my1",
+        "s": "lx0 lx1 lx2 lp lvq lvp lwq lwp lab dl dc0 dc2 dc1 ds2 ds3 ds0 dy1",
+        "g": "ipcol ik16 ijm16 ik4 irow sl0.0 sq0.0 sp0.0 sq1.0 sp1.0 sl0.1 sq0.1 sp0.1 sq1.1 sp1.1",
+    },
+    1: {
+        "v": "pi2 pi1 pi0 pf uoff pg fx0 jw ka16 qu kb16 puc id1 qx0 kk16 qx1 fx3 id0 qx2 dd wz pro fd sv2.0 jw2 vb0.0 vb1.0 wb0.0 wb1.0 cw.0 o0.0 tn1.0 tm.0 tn0.0 tn2.0 to.0 b1.0 b3.0 b2.0 ou1.0 ou2.0 g20.0 g30.0 g41.0 o4i s11.0 s12.0 o41.0 s10.0 o42.0 o40.0 g52.0 s41.0 s42.0 s40.0 la.0 of2.0 lb.0 of3.0 lc2.0 lc3.0 of1.0 lr1.0 lr0.0 qa of0.0 y02.0 y03.0 y11.0 qy0.0 qy1.0 pk0c.0 pk1c.0 av00.0 av03.0 av12.0 mx00.0 mx01.0 mx02.0 mx03.0 mx10.0 mx12.0 mx13.0 mx11.0 qn0.0 x20.0 x21.0 qn1.0 qn2.0 sv0.1 nv1.1 nv2.1 vb0.1 vb1.1 wb0.1 wb1.1 cw.1 tm.1 o0.1 tn0.1 tn2.1 tn1.1 to.1 b1.1 b2.1 ou1.1 b3.1 g21.1 ou2.1 g31.1 g40.1 s10.1 s11.1 o40.1 s12.1 o41.1 o42.1 g51.1 s40.1 s41.1 s42.1 la.1 of3.1 lb.1 of1.1 lc3.1 lc2.1 of2.1 of0.1 lr1.1 lr0.1 y02.1 qy0.1 y12.1 y11.1 qy1.1 pk0c.1 pk1p.1 pk1c.1 av03.1 av02.1 mx00.1 mx03.1 av13.1 mx01.1 mx02.1 mx11.1 mx12.1 mx13.1 mx10.1 x20.1 x10.1 qn2.1 qn0.1 qn1.1 ys0 ys1",
+        "a": "lu fx1 e0 fx2 pup sv0.0 nv0.0 sv1.0 nv1.0 nv2.0 g10.0 g21.0 g31.0 g42.0 g40.0 g51.0 g50.0 y12.0 y13.0 y00.0 y01.0 y10.0 pk0p.0 pk1p.0 av01.0 av02.0 av10.0 av13.0 av11.0 x00.0 x01.0 x10.0 x11.0 nv0.1 sv1.1 sv2.1 g10.1 g20.1 g30.1 g41.1 g42.1 g50.1 g52.1 y03.1 y01.1 y00.1 y10.1 y13.1 pk0p.1 ol1 ol0 av00.1 av01.1 av11.1 av10.1 av12.1 x00.1 x01.1 x21.1 x11.1 dl dc0 ys2 dy2 dy1",
+        "p": "ms0.0 mt0.0 ms1.0 ms2.0 mt1.0 mt2.0 mv00.0 mv01.0 mv03.0 mv02.0 mv10.0 mv12.0 mw00.0 mw01.0 mw02.0 mv13.0 mw03.0 mv11.0 mw10.0 mw12.0 mw13.0 mw11.0 mt0.1 ms0.1 ms1.1 mt1.1 ms2.1 mt2.1 mv03.1 mv02.1 mv00.1 mv13.1 mv10.1 mv01.1 mv11.1 mw00.1 mw03.1 mv12.1 mw01.1 mw02.1 mw11.1 mw10.1 mw12.1 mw13.1 my2 my0 my1",
+        "s": "lx0 lx1 lx2 lp lvq lvp lwq lwp lab dc2 ds1 dc1 ds2 ds3 ds0 dy0",
+        "g": "ipcol ik16 ijm16 ik4 irow sl0.0 sq0.0 sp0.0 sq1.0 sp1.0 sl0.1 sq0.1 sp0.1 sq1.1 sp1.1",
+    },
+    2: {
+        "v": "pi0 pi1 pi2 pf fx0 pg jw uoff ka16 qu kb16 puc id1 o4i qx0 kk16 qx1 wz fx3 qx2 dd pro fd sv2.0 jw2 vb0.0 vb1.0 wb0.0 wb1.0 cw.0 id0 o0.0 tn1.0 tn2.0 tm.0 tn0.0 to.0 b1.0 b2.0 b3.0 ou1.0 ou2.0 g20.0 g30.0 qa g42.0 s10.0 s12.0 s11.0 o40.0 o42.0 o41.0 g52.0 s40.0 s42.0 s41.0 la.0 lb.0 lc3.0 lc2.0 of2.0 lr0.0 lr1.0 y12.0 of3.0 of0.0 y13.0 y00.0 of1.0 y02.0 qy0.0 qy1.0 pk0c.0 pk1c.0 av03.0 av01.0 mx00.0 mx01.0 mx03.0 mx02.0 mx10.0 mx11.0 mx13.0 mx12.0 x03.0 x02.0 x12.0 qn0.0 x22.0 qn1.0 qn2.0 sv0.1 sv2.1 vb0.1 vb1.1 wb0.1 wb1.1 cw.1 o0.1 tm.1 tn1.1 tn2.1 tn0.1 to.1 b1.1 b2.1 b3.1 ou1.1 ou2.1 g20.1 g30.1 g40.1 g42.1 s10.1 s11.1 s12.1 o40.1 o41.1 o42.1 g51.1 s40.1 s41.1 s42.1 la.1 of0.1 lb.1 of3.1 of2.1 lc2.1 lc3.1 of1.1 lr1.1 lr0.1 y03.1 y11.1 qy0.1 y12.1 qy1.1 pk0c.1 pk1c.1 av01.1 av00.1 av02.1 av11.1 mx01.1 mx00.1 mx02.1 mx03.1 mx10.1 mx11.1 mx12.1 mx13.1 x10.1 qn1.1 qn0.1 qn2.1 pf2c pf1c pf0c pf2p ys1 ys0",
+        "a": "lu fx1 fx2 pup sv0.0 nv0.0 e0 sv1.0 nv2.0 nv1.0 g10.0 g21.0 g31.0 g40.0 g41.0 g50.0 g51.0 y03.0 y01.0 y11.0 y10.0 pk0p.0 pk1p.0 av00.0 av10.0 av02.0 av13.0 av11.0 av12.0 x20.0 x00.0 x01.0 x10.0 x11.0 x21.0 x13.0 x23.0 nv0.1 sv1.1 nv1.1 nv2.1 g10.1 g21.1 g31.1 g41.1 g50.1 g52.1 y00.1 y02.1 y01.1 y13.1 y10.1 ok1 pk0p.1 pk1p.1 ok0 av03.1 av10.1 ol1 av12.1 av13.1 x00.1 x01.1 x11.1 x21.1 x20.1 ol0 pf1p pf0p dc1 dc0 ys2",
+        "p": "ms0.0 mt0.0 ms1.0 ms2.0 mt2.0 mt1.0 mv03.0 mv00.0 mv01.0 mv10.0 mv02.0 mv13.0 mw03.0 mw00.0 mw01.0 mv11.0 mv12.0 mw02.0 mw10.0 mw11.0 mw12.0 mw13.0 ms0.1 mt0.1 ms1.1 ms2.1 mt1.1 mt2.1 mv01.1 mv00.1 mv03.1 mv02.1 mv11.1 mv10.1 mw01.1 mw00.1 mv12.1 mw02.1 mw03.1 mv13.1 mw10.1 mw11.1 mw12.1 mw13.1 my1 my0 my2",
+        "s": "lx0 lx1 lx2 lp lvq lvp lwq lwp lab dl dc2 ds3 dy1 ds2 ds0 ds1 dy0 dy2",
+        "g": "ipcol ik4 ik16 ijm16 irow sl0.0 sq0.0 sp0.0 sq1.0 sp1.0 sl0.1 sq0.1 sp0.1 sq1.1 sp1.1",
+    },
+    3: {
+        "v": "pi0 pi1 pi2 pf ka16 fx0 uoff jw kb16 id0 qu wz fx2 puc id1 kk16 qx0 kb4 qx1 ka4 qx2 o4i dd nv0.0 fd nv1.0 pro jw2 nv2.0 vb0.0 vb1.0 wb0.0 wb1.0 cw.0 tn0.0 o0.0 to.0 tn1.0 tm.0 tn2.0 b1.0 b3.0 b2.0 ou1.0 ou2.0 g21.0 g31.0 g42.0 fx3 kk4 s11.0 s10.0 o41.0 s12.0 o40.0 o42.0 g52.0 s40.0 s41.0 of0.0 of1.0 y00.0 s42.0 qy0.0 of2.0 y11.0 qy1.0 qa pk0c.0 pk1c.0 La0.0 La1.0 av03.0 mx01.0 mx00.0 mx03.0 mx02.0 s20.0 mx12.0 mx10.0 mx11.0 s21.0 mx13.0 bw.0 x03.0 x01.0 x21.0 qn0.0 x20.0 qn1.0 qn2.0 sv2.1 vb0.1 vb1.1 wb0.1 wb1.1 cw.1 o0.1 tn2.1 tn0.1 tn1.1 tm.1 to.1 b1.1 b3.1 b2.1 ou1.1 ou2.1 g21.1 g31.1 g41.1 s10.1 s11.1 o40.1 s12.1 o41.1 o42.1 g51.1 s40.1 s41.1 of0.1 of1.1 s42.1 y00.1 of2.1 qy0.1 y11.1 qy1.1 La0.1 pk0c.1 pk1c.1 ok1 Lb0.1 av03.1 av02.1 mx00.1 mx01.1 mx02.1 mx03.1 mx11.1 mx10.1 mx12.1 mx13.1 s20.1 s21.1 x21.1 bw.1 qn0.1 qn2.1 qn1.1 pf1c pf0c pf2c pf2p ys1 ys0",
+        "a": "lu pg e0 pup sv0.0 fx1 sv2.0 sv1.0 g10.0 g20.0 g30.0 g41.0 g40.0 g51.0 g50.0 y01.0 y10.0 pk0p.0 pk1p.0 av01.0 av00.0 av02.0 av12.0 Lb0.0 av10.0 av11.0 av13.0 Lb1.0 x02.0 x00.0 x10.0 x11.0 sv0.1 nv0.1 sv1.1 nv1.1 nv2.1 g10.1 g20.1 g30.1 g40.1 g42.1 g50.1 g52.1 y01.1 y10.1 La1.1 pk0p.1 pk1p.1 ok0 av00.1 av01.1 Lb1.1 av11.1 av12.1 av10.1 av13.1 x01.1 x00.1 x20.1 x11.1 x10.1 ol0 pf1p pf0p ol1 ds2 dy1 ys2 dy0 ds1",
+        "p": "mt0.0 ms0.0 ms1.0 mt1.0 ms2.0 mt2.0 mv01.0 mv00.0 mv02.0 mv03.0 mv12.0 mv10.0 mw01.0 mw00.0 mw03.0 mw02.0 mv11.0 mw12.0 mv13.0 mw10.0 mw11.0 mw13.0 ms0.1 mt0.1 ms1.1 ms2.1 mt2.1 mt1.1 mv00.1 mv02.1 mv01.1 mv03.1 mv11.1 mv12.1 mw00.1 mw01.1 mv10.1 mv13.1 mw02.1 mw03.1 mw11.1 mw10.1 mw12.1 mw13.1 my1 my0 my2",
+        "s": "lx0 lx1 lx2 lp lvq lvp lwq lwp lab dc1 dc0 dc2 dl ds3 ds0 dy2",
+        "g": "ipcol ijm16 ik16 ijm4 irow sq0.0 sq1.0 sp1.0 sq0.1 sq1.1 sp1.1",
+    },
+}
 
 
 def _scratch():
@@ -21,27 +66,29 @@ def _scratch():
         sb(n, 128, X4)
     for n in ("us", "us2", "asc"):
         sb(n, 128, "uint8")
-    for n in ("vq", "wq"):
+    for n in ("vq", "wq", "fq"):
         sb(n, C, X4)
-    for n in ("vp", "wp"):
+    for n in ("vp", "wp", "fp"):
         sb(n, C, "uint8")
-    sb("pri", 32, "int32"); sb("pro", 32, "uint16"); sb("dd", 32, "float32")
-    sb("pcol", 2, "int32"); sb("pand", 2, "int32"); sb("pm", 2, "float32")
-    sb("k16", 32, "float32"); sb("jw", 32, "float32"); sb("uoff", 8, "uint16")
-    sb("jm", C, "float32"); sb("row", C, "float32"); sb("mbig", C, "float32")
-    sb("mask", C, "bfloat16"); sb("rst", C, "bfloat16")
-    sb("sv", C, "float32"); sb("thr", C, "float32"); sb("vb", C, "bfloat16"); sb("wb", C, "bfloat16")
-    sb("t1", 32, "float32"); sb("cw", 32, "float32"); sb("o0", 32, "uint16"); sb("o4", 32, "uint16")
+    sb("pri", 32, "int32"); sb("pro", 32, "uint16"); sb("e3", 96, "float32"); sb("fd", 32, "float32")
+    sb("pcol", 2, "int32"); sb("pi", 4, "int32"); sb("pf", 4, "float32"); sb("pg", 2, "float32"); sb("fx", 4, "float32")
+    sb("k4", 4, "float32"); sb("f4", 4, "float32"); sb("k16", 32, "float32"); sb("jw", 32, "float32"); sb("uoff", 8, "uint16")
+    for n in ("jm16", "jm4", "ka16", "kb16", "ka4", "kb4", "kk16", "kk4"):
+        sb(n, H, "bfloat16")
+    sb("sv", C, "float32"); sb("nv", C, "float32"); sb("vb", C, "bfloat16")
+    sb("wb", 3 * C, "float16"); sb("cw", 96, "float32"); sb("o0", 32, "uint16"); sb("o4", 32, "uint16")
     sb("asm", 96, "float32"); sb("bt", 96, "float32"); sb("ou", 96, "uint16")
-    for n in ("ta", "tb", "t7", "t8", "t9", "la", "lb", "ysb"):
+    for n in ("row", "r1", "r2", "r3", "r4", "r5", "la", "lb", "lc", "t8"):
+        sb(n, C, "bfloat16")
+    for n in ("t9", "ysb"):
         sb(n, C, "float32")
-    for n in ("tm", "ts", "tm2", "ts2", "tm4", "ts4"):
-        sb(n, C, LT)
-    sb("sa", 32, LT); sb("sc", 32, LT)
+    for n in ("s1", "s4", "s2"):
+        sb(n, C, "float16")
+    sb("sa", 32, "float16"); sb("sc", 32, "float16")
     for t in range(R + 1):
         sb("x%d" % t, 4 * C, "bfloat16"); sb("xq%d" % t, C, X4); sb("xs%d" % t, C, "uint8")
     for t in range(R):
-        sb("off%d" % t, 128, "uint16"); sb("lr%d" % t, 96, "uint16"); sb("bw%d" % t, 32, "uint16")
+        sb("off%d" % t, 128, "uint16"); sb("lr%d" % t, 96, "uint16"); sb("bw%d" % t, 128, "uint16")
         sb("yt%d" % t, 4 * C, "bfloat16")
         for n in ("y", "z", "k"):
             sb("%sq%d" % (n, t), C, X4); sb("%sp%d" % (n, t), C, "uint8")
@@ -52,56 +99,423 @@ def _scratch():
 
 
 SCRATCH = _scratch()
-SEMAPHORES = (["cv", "ca", "cp", "cg", "sent", "outs"] + ["ld%d" % i for i in range(9)]
-              + ["lst%d_%d" % (t, k) for t in range(R) for k in range(3)] + ["dat%d_%d" % (t, h) for t in range(R) for h in range(2)])
+SEMAPHORES = (["cv", "ca", "cp", "cg", "sent", "outs"] + ["ld%d" % i for i in range(12)]
+              + ["lst%d_%d" % (t, k) for t in range(R) for k in range(3)] + ["dat%d_%d" % (t, h) for t in range(R) for h in range(4)])
 
 
-def _list_masks(topo, src, dsts):
+def _list_masks(topo, src, dsts, busy):
     eng = {d: topo.engines(src, d) for d in dsts}
     few = min(len(e) for e in eng.values())
     narrow = [d for d in dsts if len(eng[d]) == few]
     used, out = set(), {}
     for d in narrow + [d for d in dsts if d not in narrow]:
-        free = [e for e in eng[d] if e not in used]
+        free = [e for e in eng[d] if e not in used][::-1]
         want = few // len(narrow) if d in narrow else len(free)
         n = 1
-        while 2 * n <= min(want, len(free)):
+        while 2 * n <= min(want, len(free), busy):
             n *= 2
         used.update(free[:n])
         out[d] = free[:n]
     return out
 
 
-def rank_program(g, core, T, topo):
+def rg(name, c0=0, c1=None, step=1, p0=0, p1=128):
+    return (name, p0, p1, c0, SCRATCH[name][1][1] if c1 is None else c1, step)
+
+
+def meet(x, y):
+    if x[0] != y[0]:
+        return False
+    if x[0].startswith("ps"):
+        return True
+    if x[2] <= y[1] or y[2] <= x[1] or x[4] <= y[3] or y[4] <= x[3]:
+        return False
+    if x[5] == 1 and y[5] == 1:
+        return True
+    return bool(set(range(x[3], x[4], x[5])) & set(range(y[3], y[4], y[5])))
+
+
+def runs(cut):
+    return list(zip(cut, cut[1:]))
+
+
+def parts(a, b, n):
+    return runs([a + (b - a) * i // n for i in range(n + 1)])
+
+
+def plan(g, core, T, topo):
     r = T.rank_of(core)
-    if r is None:
-        return
     cores = T.cores
     N = len(cores)
     Q = {"v": g.vector, "a": g.scalar, "p": g.tensor, "s": g.sync, "g": g}
-    CS = {"v": "cv", "a": "ca", "p": "cp", "g": "cg"}
-    cnt, known, waited, hist = {}, {q: {} for q in Q}, {}, []
-    ADD, MUL, SUB = AluOpType.add, AluOpType.mult, AluOpType.subtract
-    COPY = ActivationFunctionType.Copy
+    ADD, MUL, SUB, MIN = AluOpType.add, AluOpType.mult, AluOpType.subtract, AluOpType.min
+    COPY, IDENT = ActivationFunctionType.Copy, ActivationFunctionType.Identity
     HALVES = ((0, H), (H, C))
-
-    def rg(name, c0=0, c1=None, step=1, p0=0, p1=128):
-        return (name, p0, p1, c0, SCRATCH[name][1][1] if c1 is None else c1, step)
+    calls, lands, tag = [], [], [""]
 
     def ap(x):
         n, p0, p1, c0, c1, st = x
         return T[n][p0:p1, c0:c1] if st == 1 else T[n][p0:p1, c0:c1:st]
 
-    def meet(x, y):
-        if x[0] != y[0]:
-            return False
-        if x[0].startswith("ps"):
-            return True
-        if x[2] <= y[1] or y[2] <= x[1] or x[4] <= y[3] or y[4] <= x[3]:
-            return False
-        if x[5] == 1 and y[5] == 1:
-            return True
-        return bool(set(range(x[3], x[4], x[5])) & set(range(y[3], y[4], y[5])))
+    def op(name, qs, fn, reads, writes, kind="op"):
+        calls.append((name + tag[0], qs, kind, fn, reads, writes))
+
+    def dma(name, qs, sem, out, in_, reads, writes):
+        op(name, qs, lambda q: Q[q].dma_start(out, in_), reads, writes, ("dma", sem))
+
+    def move(name, qs, out, in_, off=None, mul=None, add=None):
+        def fn(q):
+            i = ap(in_) if off is None else ap(in_).indirect(ap(off))
+            if q == "a":
+                if add is not None:
+                    return g.scalar.activation(ap(out), i, IDENT, bias=add)
+                if mul is not None:
+                    return g.scalar.activation(ap(out), i, COPY, scale=mul)
+                return g.scalar.activation(ap(out), i, COPY)
+            if add is not None:
+                return g.vector.tensor_scalar(ap(out), i, add, None, ADD)
+            if mul is not None:
+                return g.vector.tensor_scalar(ap(out), i, mul, None, MUL)
+            return g.vector.tensor_copy(ap(out), i)
+        op(name, qs, fn, [in_] + ([] if off is None else [off]), [out])
+
+    def sub(lst, a, b):
+        return rg(lst[0], lst[3] + a // 16, lst[3] + b // 16)
+
+    def compose(name, out, win, lst, cut=HALVES, add=None):
+        for i, (a, b) in enumerate(cut):
+            move("%s%d" % (name, i), "av", rg(out, a, b), rg(win), sub(lst, a, b), add=add)
+
+    def tt(name, out, a, b, alu, off=None):
+        if off is None:
+            op(name, "v", lambda q: g.vector.tensor_tensor(ap(out), ap(a), ap(b), alu), [a, b], [out])
+        else:
+            op(name, "v", lambda q: g.vector.tensor_tensor(ap(out), ap(a).indirect(ap(off)), ap(b), alu), [a, b, off], [out])
+
+    def ts(name, out, a, s1, op0, s2=None, op1=None):
+        col = [s for s in (s1, s2) if isinstance(s, tuple)]
+        v1, v2 = [ap(s) if isinstance(s, tuple) else s for s in (s1, s2)]
+        if op1 is None:
+            op(name, "v", lambda q: g.vector.tensor_scalar(ap(out), ap(a), v1, None, op0), [a] + col, [out])
+        else:
+            op(name, "v", lambda q: g.vector.tensor_scalar(ap(out), ap(a), v1, v2, op0, op1), [a] + col, [out])
+
+    def tr(name, out, in_):
+        op(name, "v", lambda q: g.vector.transpose(ap(out), ap(in_)), [in_], [out])
+
+    def scan(name, out, d0, d1, op0, op1):
+        op(name, "v", lambda q: g.vector.tensor_tensor_scan(ap(out), ap(d0), ap(d1), 0.0, op0, op1), [d0, d1], [out])
+
+    def wrap(name, out, row, steps, cut, p1=128, step=1):
+        for i, (a, b) in enumerate(cut):
+            scan("%s%d" % (name, i), rg(out, step * a, step * b, step, 0, p1), rg(steps, 0, b - a, 1, 0, p1), rg(row, a, b, 1, 0, p1), ADD, MIN)
+
+    def quant(name, q_, s, tile, a, b):
+        o1, o2, i = rg(q_, a, b), rg(s, a, b), rg(tile, 4 * a, 4 * b)
+        op(name, "v", lambda q: g.vector.quantize_mx(ap(o1), ap(o2), ap(i)), [i], [o1, o2])
+
+    def mm(name, bank, wq, ws, w0, xq, xs, a, b):
+        o, i = rg("ps%d" % bank, 0, b - a), [rg(wq, w0, w0 + 128), rg(ws, w0, w0 + 128), rg(xq, a, b), rg(xs, a, b)]
+        op(name, "p", lambda q: g.tensor.matmul_mx(ap(o), ap(i[0]), ap(i[1]), ap(i[2]), ap(i[3]), True, True), i, [o])
+
+    def pick(name, oq, op_, iq, ip, off):
+        op(name + "c", "v", lambda q: g.vector.tensor_copy(ap(oq).bitcast(dt.uint32), ap(iq).bitcast(dt.uint32).indirect(ap(off))), [iq, off], [oq])
+        move(name + "p", "av", op_, ip, off)
+
+    def iota(name, pattern, base, cm, flt):
+        out = rg(name)
+        if flt:
+            op("i" + name, "g", lambda q: g.iota(ap(out), pattern, base, cm, allow_small_or_imprecise_dtypes=True), [], [out])
+        else:
+            op("i" + name, "g", lambda q: g.iota(ap(out), pattern, base, cm), [], [out])
+
+    def col(name, j, p0=0, p1=128):
+        return rg(name, j, j + 1, 1, p0, p1)
+
+    def full(src, dst):
+        return topo.mask(cores[src], cores[dst]), len(topo.engines(cores[src], cores[dst]))
+
+    def list_engines(k, dsts):
+        return _list_masks(topo, cores[k], [cores[d] for d in dsts], min(full(i, (i + 1) % N)[1] for i in range(N)))
+
+    nxt, prv = (r + 1) % N, (r - 1) % N
+    xcut = PAR["xcut"][r]
+    four = r == N - 1
+
+    dma("lu", "as", "ld1", ap(rg("ub")), T.u[:, :], [], [rg("ub")])
+    for i, (a, b) in enumerate(runs(xcut[0])):
+        dma("lx%d" % i, "sa", "ld%d" % (8 + i), ap(rg("x0", 4 * a, 4 * b)), T.x[:, 4 * a:4 * b], [], [rg("x0", 4 * a, 4 * b)])
+    dma("lp", "as", "ld0", ap(rg("pri")), T.pr[:, :], [], [rg("pri")])
+    dma("lvq", "s", "ld4", ap(rg("vq")).bitcast(dt.uint8), T.vc[:, :], [rg("x0")], [rg("vq")])
+    dma("lvp", "s", "ld5", ap(rg("vp")), T.vs[:, :], [rg("x0")], [rg("vp")])
+    dma("lwq", "s", "ld6", ap(rg("wq")).bitcast(dt.uint8), T.wc[:, :], [rg("x0")], [rg("wq")])
+    dma("lwp", "s", "ld7", ap(rg("wp")), T.ws[:, :], [rg("x0")], [rg("wp")])
+    dma("lab", "s", "ld2", ap(rg("ab")), T.a[:, :], [rg("x0")], [rg("ab")])
+
+    iota("k16", [[16, 32]], 0, 0, True)
+    iota("pcol", [[0, 2]], 0, 1, False)
+    iota("jm16", [[0, H // 16], [1, 16]], 0, 0, True)
+    iota("row", [[1, C]], -int(MID), 0, True)
+    if four:
+        iota("jm4", [[0, H // 4], [1, 4]], 0, 0, True)
+    else:
+        iota("k4", [[1, 4]], 0, 0, True)
+    move("uoff", "v", rg("uoff"), rg("k16", 0, 8))
+    ts("pi0", col("pi", 0), col("pcol", 0), 15, AluOpType.bitwise_and)
+    ts("pi1", col("pi", 1), col("pcol", 0), 2, AluOpType.arith_shift_right, 3, AluOpType.bitwise_and)
+    ts("pi2", col("pi", 2), col("pcol", 0), 3, AluOpType.bitwise_and)
+    move("pf", "v", rg("pf", 0, 3), rg("pi", 0, 3))
+    move("pg", "va", rg("pg"), rg("pf", 0, 2), add=1.0)
+    ts("fx0", col("fx", 0), col("pf", 0), 15.0, AluOpType.is_lt, -DOWN, MUL)
+    move("fx1", "va", col("fx", 1), col("fx", 0), add=MID)
+    if four:
+        ts("fx2", col("fx", 2), col("pf", 1), 3.0, AluOpType.is_lt, -4.0 * DOWN, MUL)
+        ts("fx3", col("fx", 3), col("fx", 2), col("pf", 2), ADD, 4.0 * MID, ADD)
+    else:
+        move("fx2", "va", col("fx", 2), col("fx", 1), mul=4.0)
+        ts("fx3", rg("f4"), rg("k4"), col("fx", 2), ADD)
+    ts("jw", rg("jw"), rg("k16"), col("pf", 0), ADD)
+    for k in range(2):
+        tr("id%d" % k, rg("asm", 32 * k, 32 * k + 32), rg("jw"))
+    move("o4i", "v", rg("o4", 0, 32, 1, 0, 64), rg("jw", 0, 32, 1, 0, 64))
+    for j, n in enumerate(("16", "4") if four else ("16",)):
+        ts("ka" + n, rg("ka" + n), rg("jm" + n), col("pf", j), AluOpType.is_equal, UP, MUL)
+        ts("kb" + n, rg("kb" + n), rg("jm" + n), col("pg", j), AluOpType.is_equal, DOWN / UP, MUL)
+        scan("kk" + n, rg("kk" + n), rg("kb" + n), rg("ka" + n), MUL, ADD)
+    quant("qu", "uq", "us", "ub", 0, 128)
+    pick("pu", rg("uq2"), rg("us2"), rg("uq"), rg("us"), rg("uoff"))
+    move("pro", "v", rg("pro"), rg("pri"))
+    move("e0", "va", rg("e3", 0, 96, 3), rg("jw"))
+    ts("wz", rg("wb", 13, 3 * C, 16), rg("jm16", 0, 96), 0.0, MUL)
+    tt("dd", rg("e3", 1, 96, 3), rg("pri"), rg("jw"), SUB)
+    ts("fd", rg("fd"), rg("e3", 1, 96, 3), col("fx", 0), MUL)
+    tt("jw2", rg("e3", 2, 96, 3), rg("fd"), rg("jw"), ADD)
+    for i, (a, b) in enumerate(runs(xcut[0])):
+        quant("qx%d" % i, "xq0", "xs0", "x0", a, b)
+    quant("qa", "aq", "asc", "ab", 0, 128)
+
+    for t in range(R):
+        tag[0] = "." + str(t)
+        last = t == R - 1
+        X, xq, xs = "x%d" % t, "xq%d" % t, "xs%d" % t
+        X2, xq2, xs2 = "x%d" % (t + 1), "xq%d" % (t + 1), "xs%d" % (t + 1)
+        off, lr, bw = "off%d" % t, "lr%d" % t, "bw%d" % t
+        Y, yq, yp, zq, zp, kq, kp = ["%s%d" % (n, t) for n in ("yt", "yq", "yp", "zq", "zp", "kq", "kp")]
+        av, mx = "av%d" % t, "mx%d" % t
+
+        def L(k):
+            return rg(lr, 32 * k, 32 * k + 32)
+
+        for k in range(N):
+            for dsts in PAR["lists"][k]:
+                if r in dsts:
+                    lands.append(("lst%d_%d" % (t, k), len(list_engines(k, dsts)[core]), [L(k)]))
+        ne = full(prv, r)[1]
+        zrun = runs(PAR["ycut"][prv])
+        for h, (a, b) in enumerate(zrun):
+            if not PAR["whole"][prv]:
+                lands.append(("dat%d_%d" % (t, h), 2 * ne, [rg(zq, a, b), rg(zp, a, b)]))
+            elif h < len(zrun) - 1:
+                lands.append(("dat%d_%d" % (t, h), ne, [rg(zq, a, b)]))
+            else:
+                lands.append(("dat%d_%d" % (t, h), 2 * ne, [rg(zq, a, b), rg(zp)]))
+
+        for i, (a, b) in enumerate(runs(xcut[t])):
+            mm("ms%d" % i, i, "uq2", "us2", 0, xq, xs, a, b)
+            mm("mt%d" % i, 4 + i, "uq2", "us2", 0, xq, xs, a, b)
+            move("sv%d" % i, "av", rg("sv", a, b), rg("ps%d" % i, 0, b - a))
+            move("nv%d" % i, "va", rg("nv", a, b), rg("ps%d" % (4 + i), 0, b - a), mul=-1.0)
+        for i, (a, b) in enumerate(runs(PAR["vcut"])):
+            tt("vb%d" % i, rg("vb", a, b), rg("sv"), rg("nv", a, b), AluOpType.is_gt, sub(rg("pro"), a, b))
+        wrap("wb", "wb", "vb", "kk16", runs(PAR["vcut"]), 128, 3)
+        scan("cw", rg("cw"), rg("wb", 13, 3 * C, 16), rg("e3"), MUL, ADD)
+
+        def cw(p0=0, p1=128):
+            return rg("cw", 2, 96, 3, p0, p1)
+        move("o0", "v", rg("o0"), cw())
+        tr("tm", rg("asm", 64, 96), cw())
+        for a in range(3):
+            tr("tn%d" % a, rg("asm", 32, 64, 1, 32 * a + 32, 32 * a + 64), cw(32 * a, 32 * a + 32))
+        tr("to", rg("asm", 0, 32, 1, 64, 128), cw(0, 64))
+        for i in range(3):
+            tr("b%d" % (i + 1), rg("bt", 32 * i, 32 * i + 32), rg("asm", 48 - 16 * i, 80 - 16 * i))
+        move("ou1", "v", rg("ou", 0, 32), rg("bt", 0, 32))
+        move("ou2", "v", rg("ou", 32, 96), rg("bt", 32, 96))
+
+        W = runs(PAR["wcut"])
+        compose("g1", "r1", "row", rg("o0"), ((0, C),))
+        compose("g2", "r2", "r1", rg("ou", 0, 32))
+        compose("g3", "r3", "r2", rg("ou", 32, 64))
+        compose("g4", "r4", "r3", rg("ou", 64, 96), W)
+        wrap("s1", "s1", "r4", "kk16", W, 64)
+        for i, (a, b) in enumerate(W):
+            ts("o4%d" % i, rg("o4", a // 16, b // 16, 1, 64, 128), rg("s1", a + 15, b, 16, 0, 64), col("fx", 1, 0, 64), ADD)
+        compose("g5", "r5", "r4", rg("o4"), W)
+        if four:
+            wrap("s4", "s4", "r5", "kk4", W)
+            for i, (a, b) in enumerate(W):
+                ts("of%d" % i, rg(off, a // 4, b // 4), rg("s4", a + 3, b, 4), 4.0, MUL, col("fx", 3), ADD)
+        else:
+            wrap("s4", "s4", "r5", "kk16", W)
+            for k in range(4):
+                ts("of%d" % k, rg(off, 32 * k, 32 * k + 32), rg("s4", 15, C, 16), 4.0, MUL, col("f4", k), ADD)
+            tr("la", rg("sa", 0, 32, 1, 96, 128), rg("s4", 15, C, 16, 96, 128))
+            move("lb", "v", rg("sa", 0, 16, 1, 96, 128), rg("sa", 16, 32, 1, 96, 128))
+            for q in (2, 3):
+                tr("lc%d" % q, rg("sc", 0, 32, 1, 32 * q, 32 * q + 32), rg("sa", 0, 32, 1, 96, 128))
+            for q in range(2):
+                ts("lr%d" % q, rg(lr, 32 * r, 32 * r + 32, 1, 64 * q, 64 * q + 64), rg("sc", 0, 32, 1, 64, 128), col("fx", 1, 64, 128), ADD)
+        for i, dsts in enumerate(PAR["lists"][r]):
+            em, trs = list_engines(r, dsts), []
+            for d in dsts:
+                rid, pid, _ = topo.addr(cores[d])
+                trs.append(RemoteDMATransfer(dst_ids=[DstId(rid=rid, pnc=pid)], dma_engine_mask=sum(1 << e for e in em[cores[d]]),
+                                             remote_sem=T.sem["lst%d_%d" % (t, r)], src=ap(L(r)), dst=ap(L(r))))
+            op("sl%d" % i, "g", lambda q, trs=trs: g.remote_dma_fused(trs, local_sem=T.sem.sent), [L(r)], [],
+               ("far", sum(len(e) for e in em.values())))
+
+        rid, pid, _ = topo.addr(cores[nxt])
+        msk, ne = full(r, nxt)
+
+        def send(name, out, in_, h, codes):
+            o, i = (ap(out).bitcast(dt.uint8), ap(in_).bitcast(dt.uint8)) if codes else (ap(out), ap(in_))
+            sem = T.sem["dat%d_%d" % (t, h)]
+            op(name, "g", lambda q, pid=pid, rid=rid, msk=msk: g.remote_dma(o, i, sem, T.sem.sent, pid, rid, msk), [in_], [], ("far", ne))
+
+        yrun = runs(PAR["ycut"][r])
+        for h, (a, b) in enumerate(yrun):
+            if four:
+                m = 4 * a + 32 * ((b - a) * PAR["yshare"] // 256)
+                for i, (c, d) in enumerate(((4 * a, m), (m, 4 * b))):
+                    move("y%d%d" % (h, i), "av", rg(Y, c, d), rg(X), sub(rg(off), c, d))
+            else:
+                for i in range(4):
+                    move("y%d%d" % (h, i), "av", rg(Y, 4 * a + i, 4 * b, 4), rg(X), sub(rg(off, 32 * i), a, b))
+            quant("qy%d" % h, yq, yp, Y, a, b)
+            send("sq%d" % h, rg(zq, a, b), rg(yq, a, b), h, True)
+            if not PAR["whole"][r]:
+                send("sp%d" % h, rg(zp, a, b), rg(yp, a, b), h, False)
+            elif h == len(yrun) - 1:
+                send("sp%d" % h, rg(zp), rg(yp), h, False)
+
+        sets = [1]
+
+        def banks():
+            sets[0] += 1
+            return 4 * (sets[0] % 2)
+
+        def vprod(h, q_, p_, a, b):
+            k = banks()
+            for i in range(4):
+                mm("mv%d%d" % (h, i), k + i, "vq", "vp", 128 * i, q_, p_, a, b)
+                move("av%d%d" % (h, i), "av", rg(av, C * i + a, C * i + b), rg("ps%d" % (k + i), 0, b - a))
+
+        back = None
+        if r == 0:
+            for h, (a, b) in enumerate(HALVES):
+                vprod(h, yq, yp, a, b)
+            compose("La", "la", "row", L(2))
+            compose("Lb", "lb", "la", L(1))
+            compose("Lc", "lc", "lb", L(0), runs(PAR["bcut"]))
+            wrap("s2", "s2", "lc", "kk16", runs(PAR["bcut"]))
+            for i, (a, b) in enumerate(runs(PAR["bcut"])):
+                ts("bw%d" % i, rg(bw, a // 16, b // 16), rg("s2", a + 15, b, 16), col("fx", 1), ADD)
+            wrun = runs(PAR["kcut"])
+            for h, (a, b) in enumerate(wrun):
+                pick("pk%d" % h, rg(kq, a, b), rg(kp, a, b), rg(zq), rg(zp), sub(rg(bw), a, b))
+            wq_, wp_ = kq, kp
+        else:
+            for h, (a, b) in enumerate(runs(PAR["pcut"])):
+                pick("pk%d" % h, rg(kq, a, b), rg(kp, a, b), rg(yq), rg(yp), sub(L(r - 1), a, b))
+                vprod(h, kq, kp, a, b)
+            wq_, wp_, wrun = zq, zp, zrun
+            if r == 2:
+                back = L(0)
+            if r == 3:
+                compose("La", "la", "row", L(1))
+                compose("Lb", "lb", "la", L(0))
+                back = rg(bw)
+                if last:
+                    wrap("s2", "s2", "lb", "kk16", HALVES)
+                    ts("bw", rg(bw, 0, 32), rg("s2", 15, C, 16), col("fx", 1), ADD)
+                else:
+                    wrap("s2", "s2", "lb", "kk4", HALVES)
+                    ts("bw", rg(bw), rg("s2", 3, C, 4), 4.0, MUL, col("fx", 3), ADD)
+
+        planes = back is not None and not four and not last
+        for h, (a, b) in enumerate(wrun):
+            k = banks()
+            for i in range(4):
+                mm("mw%d%d" % (h, i), k + i, "wq", "wp", 128 * i, wq_, wp_, a, b)
+                o = rg(mx, C * i + a, C * i + b) if planes else rg(mx, 4 * a + i, 4 * b, 4)
+                tt("mx%d%d" % (h, i), o, rg("ps%d" % (k + i), 0, b - a), rg(av, C * i + a, C * i + b), AluOpType.max)
+        for h, (a, b) in enumerate(runs(xcut[t + 1])):
+            if back is None or last:
+                for i, (c, d) in enumerate(parts(4 * a, 4 * b, 2)):
+                    move("x%d%d" % (h, i), "av", rg(X2, c, d), rg(mx, c, d), mul=SC)
+            elif planes:
+                for i in range(4):
+                    move("x%d%d" % (h, i), "av", rg(X2, 4 * a + i, 4 * b, 4), rg(mx, C * i, C * i + C), sub(back, a, b), mul=SC)
+            else:
+                for i, (c, d) in enumerate(parts(4 * a, 4 * b, (b - a) // 64)):
+                    move("x%d%d" % (h, i), "av", rg(X2, c, d), rg(mx), sub(back, c, d), mul=SC)
+            quant("qn%d" % h, xq2, xs2, X2, a, b)
+
+    tag[0] = ""
+    if r == 0:
+        move("ol", "av", rg("t9"), rg("r5"), add=MID)
+    elif r == 1:
+        compose("ol", "t9", "r5", L(0), add=MID)
+    else:
+        compose("ok", "t8", "r5", L(r - 1))
+        compose("ol", "t9", "t8", back, add=MID)
+    dma("dl", "sa", "outs", T.ol[:, :], T.t9[0:128:16, :], [rg("t9")], [])
+    xq, xs, orun = "xq%d" % R, "xs%d" % R, runs(xcut[R])
+    if back is not None:
+        orun = runs(PAR["fcut"])
+        for h, (a, b) in enumerate(orun):
+            pick("pf%d" % h, rg("fq", a, b), rg("fp", a, b), rg(xq), rg(xs), sub(back, a, b))
+        xq, xs = "fq", "fp"
+    for h, (a, b) in enumerate(orun):
+        bank = 4 * (h % 2) + h // 2
+        mm("my%d" % h, bank, "aq", "asc", 0, xq, xs, a, b)
+        dma("dc%d" % h, "sa", "outs", T.oc[:, 4 * a:4 * b], ap(rg(xq, a, b)).bitcast(dt.uint8), [rg(xq, a, b)], [])
+        move("ys%d" % h, "va", rg("ysb", a, b), rg("ps%d" % bank, 0, b - a))
+        dma("dy%d" % h, "sa", "outs", T.y[:, a:b], ap(rg("ysb", a, b)), [rg("ysb", a, b)], [])
+    for k in range(4):
+        dma("ds%d" % k, "sa", "outs", T.osc[4 * k:4 * k + 4, :], T[xs][32 * k:32 * k + 4, :], [rg(xs)], [])
+    return calls, lands
+
+
+def merge(calls, lines):
+    seen, need = {}, {}
+    for name, qs, kind, fn, reads, writes in calls:
+        need[name] = {m for y, w in [(y, True) for y in writes] + [(y, False) for y in reads] for x, wr, m in seen.get(y[0], [])
+                      if (w or wr or x[0].startswith("ps")) and meet(x, y)}
+        for x in reads:
+            seen.setdefault(x[0], []).append((x, False, name))
+        for x in writes:
+            seen.setdefault(x[0], []).append((x, True, name))
+    todo = {q: lines[q].split() for q in lines}
+    seq, done = [], set()
+    while any(todo.values()):
+        free = [q for q in todo if todo[q] and need[todo[q][0]] <= done]
+        assert free
+        for q in free:
+            done.add(todo[q][0])
+            seq.append((todo[q].pop(0), q))
+    assert done == set(need) and len(seq) == len(calls)
+    return seq
+
+
+def rank_program(g, core, T, topo):
+    r = T.rank_of(core)
+    if r is None:
+        return
+    Q = {"v": g.vector, "a": g.scalar, "p": g.tensor, "s": g.sync, "g": g}
+    CS = {"v": "cv", "a": "ca", "p": "cp", "g": "cg"}
+    cnt, known, waited, hist = {}, {q: {} for q in Q}, {}, {}
+    calls, lands = plan(g, core, T, topo)
 
     def wait(q, ev):
         sem, n, clock = ev
@@ -115,12 +529,10 @@ def rank_program(g, core, T, topo):
 
     def order(q, reads, writes):
         need = {}
-        for x, wr, ev, eq in hist:
-            hit = any(meet(x, y) for y in writes)
-            if not hit and (wr or (x[0].startswith("ps") and eq != q)):
-                hit = any(meet(x, y) for y in reads)
-            if hit and (ev[0] not in need or need[ev[0]][1] < ev[1]):
-                need[ev[0]] = ev
+        for y, w in [(y, True) for y in writes] + [(y, False) for y in reads]:
+            for x, wr, ev, eq in hist.get(y[0], []):
+                if (w or wr or (x[0].startswith("ps") and eq != q)) and meet(x, y) and (ev[0] not in need or need[ev[0]][1] < ev[1]):
+                    need[ev[0]] = ev
         evs = list(need.values())
         for ev in evs:
             if not any(o is not ev and o[2].get(ev[0], 0) >= ev[1] for o in evs):
@@ -128,364 +540,27 @@ def rank_program(g, core, T, topo):
 
     def note(q, ev, reads, writes):
         for x in reads:
-            hist.append((x, False, ev, q))
+            hist.setdefault(x[0], []).append((x, False, ev, q))
         for x in writes:
-            hist.append((x, True, ev, q))
+            hist.setdefault(x[0], []).append((x, True, ev, q))
 
-    def op(q, fn, reads, writes):
-        order(q, reads, writes)
-        sem = CS[q]
-        fn().then_inc(T.sem[sem], 1)
-        cnt[sem] = cnt.get(sem, 0) + 1
-        note(q, (sem, cnt[sem], dict(known[q])), reads, writes)
-
-    def dma(q, sem, out, in_, reads, writes):
-        order(q, reads, writes)
-        Q[q].dma_start(out, in_).then_inc(T.sem[sem], 16)
-        cnt[sem] = cnt.get(sem, 0) + 16
-        note(q, (sem, cnt[sem], dict(known[q])), reads, writes)
-
-    def lands(sem, n, writes):
+    for sem, n, writes in lands:
         cnt[sem] = n
         note("far", (sem, n, {}), [], writes)
 
-    def copy(q, out, in_, scale=None):
-        if q == "a":
-            if scale is None:
-                op(q, lambda: g.scalar.activation(ap(out), ap(in_), COPY), [in_], [out])
-            else:
-                op(q, lambda: g.scalar.activation(ap(out), ap(in_), COPY, scale=scale), [in_], [out])
-        else:
-            op(q, lambda: g.vector.tensor_copy(ap(out), ap(in_)), [in_], [out])
-
-    def gather(q, out, win, off, scale=None):
-        if q == "a":
-            if scale is None:
-                op(q, lambda: g.scalar.activation(ap(out), ap(win).indirect(ap(off)), COPY), [win, off], [out])
-            else:
-                op(q, lambda: g.scalar.activation(ap(out), ap(win).indirect(ap(off)), COPY, scale=scale), [win, off], [out])
-        elif scale is None:
-            op(q, lambda: g.vector.tensor_copy(ap(out), ap(win).indirect(ap(off))), [win, off], [out])
-        else:
-            op(q, lambda: g.vector.tensor_scalar(ap(out), ap(win).indirect(ap(off)), scale, None, MUL), [win, off], [out])
-
-    def split(out, win, offn, o):
-        gather("v", rg(out, 0, H), rg(win), rg(offn, o, o + 16))
-        gather("a", rg(out, H, C), rg(win), rg(offn, o + 16, o + 32))
-
-    def tt(out, a, b, alu, off=None):
-        if off is None:
-            op("v", lambda: g.vector.tensor_tensor(ap(out), ap(a), ap(b), alu), [a, b], [out])
-        else:
-            op("v", lambda: g.vector.tensor_tensor(ap(out), ap(a).indirect(ap(off)), ap(b), alu), [a, b, off], [out])
-
-    def ts(out, a, s1, op0, s2=None, op1=None):
-        col = [s1] if isinstance(s1, tuple) else []
-        v1 = ap(s1) if col else s1
-        if op1 is None:
-            op("v", lambda: g.vector.tensor_scalar(ap(out), ap(a), v1, None, op0), [a] + col, [out])
-        else:
-            op("v", lambda: g.vector.tensor_scalar(ap(out), ap(a), v1, s2, op0, op1), [a] + col, [out])
-
-    def tr(out, in_):
-        op("v", lambda: g.vector.transpose(ap(out), ap(in_)), [in_], [out])
-
-    def scan(out, data):
-        rst = rg("rst", data[3], data[4])
-        op("v", lambda: g.vector.tensor_tensor_scan(ap(out), ap(rst), ap(data), 0.0, MUL, ADD), [rst, data], [out])
-
-    def quant(q, s, tile, a, b):
-        o1, o2, i = rg(q, a, b), rg(s, a, b), rg(tile, 4 * a, 4 * b)
-        op("v", lambda: g.vector.quantize_mx(ap(o1), ap(o2), ap(i)), [i], [o1, o2])
-
-    def mm(bank, wq, ws, w0, xq, xs, a, b):
-        o, i = rg("ps%d" % bank, 0, b - a), [rg(wq, w0, w0 + 128), rg(ws, w0, w0 + 128), rg(xq, a, b), rg(xs, a, b)]
-        op("p", lambda: g.tensor.matmul_mx(ap(o), ap(i[0]), ap(i[1]), ap(i[2]), ap(i[3]), True, True), i, [o])
-
-    def pick_codes(out, win, off):
-        op("v", lambda: g.vector.tensor_copy(ap(out).bitcast(dt.uint32), ap(win).bitcast(dt.uint32).indirect(ap(off))), [win, off], [out])
-
-    def iota(out, pattern, base, cm, flt):
-        if flt:
-            op("g", lambda: g.iota(ap(out), pattern, base, cm, allow_small_or_imprecise_dtypes=True), [], [out])
-        else:
-            op("g", lambda: g.iota(ap(out), pattern, base, cm), [], [out])
-
-    def wrap(out, win, off, m, s, other="mask", alu=MUL):
-        for a, b in HALVES:
-            tt(rg(m, a, b), win, rg(other, a, b), alu, rg(off[0], off[3] + a // 16, off[3] + b // 16))
-        for a, b in HALVES:
-            scan(rg(s, a, b), rg(m, a, b))
-        if out is not None:
-            for a, b in HALVES:
-                copy("v", rg(out[0], a // 16, b // 16, 1, out[1], out[2]), rg(s, a + 15, b, 16, 0, out[2] - out[1]))
-
-    def list_dsts(k):
-        return [] if k == N - 1 else [d for d in range(N) if d > k or (d == 0 and k > 0)]
-
-    def full(src, dst):
-        return topo.mask(cores[src], cores[dst]), len(topo.engines(cores[src], cores[dst]))
-
-    nxt, prv = (r + 1) % N, (r - 1) % N
-
-    dma("a", "ld1", ap(rg("ub")), T.u[:, :], [], [rg("ub")])
-    dma("s", "ld2", ap(rg("x0", 0, 4 * H)), T.x[:, 0:4 * H], [], [rg("x0", 0, 4 * H)])
-    dma("s", "ld3", ap(rg("x0", 4 * H, 4 * C)), T.x[:, 4 * H:4 * C], [], [rg("x0", 4 * H, 4 * C)])
-    dma("s", "ld0", ap(rg("pri")), T.pr[:, :], [], [rg("pri")])
-    order("s", [rg("x0")], [])
-    dma("s", "ld4", ap(rg("vq")).bitcast(dt.uint8), T.vc[:, :], [], [rg("vq")])
-    dma("s", "ld5", ap(rg("vp")), T.vs[:, :], [], [rg("vp")])
-    dma("s", "ld6", ap(rg("wq")).bitcast(dt.uint8), T.wc[:, :], [], [rg("wq")])
-    dma("s", "ld7", ap(rg("wp")), T.ws[:, :], [], [rg("wp")])
-    dma("s", "ld8", ap(rg("ab")), T.a[:, :], [], [rg("ab")])
-
-    iota(rg("pcol"), [[0, 2]], 0, 1, False)
-    iota(rg("k16"), [[16, 32]], 0, 0, True)
-    iota(rg("jm"), [[0, 32], [1, 16]], 0, 0, True)
-    iota(rg("row"), [[1, C]], 0, 0, True)
-    op("v", lambda: g.vector.memset(ap(rg("rst")), 1.0), [], [rg("rst")])
-    op("v", lambda: g.vector.memset(ap(rg("rst", 0, C, 16)), 0.0), [], [rg("rst", 0, C, 16)])
-    ts(rg("pand"), rg("pcol"), 15, AluOpType.bitwise_and)
-    copy("v", rg("uoff"), rg("k16", 0, 8))
-    copy("v", rg("pm"), rg("pand"))
-    ts(rg("jw"), rg("k16"), rg("pm", 0, 1), ADD)
-    for k in range(2):
-        tr(rg("asm", 32 * k, 32 * k + 32), rg("jw"))
-    copy("v", rg("o4", 0, 32, 1, 0, 64), rg("jw", 0, 32, 1, 0, 64))
-    ts(rg("mbig"), rg("jm"), rg("pm", 0, 1), AluOpType.not_equal, BIG, MUL)
-    quant("uq", "us", "ub", 0, 128)
-    pick_codes(rg("uq2"), rg("uq"), rg("uoff"))
-    gather("a", rg("us2"), rg("us"), rg("uoff"))
-    op("a", lambda: g.scalar.activation(ap(rg("mask")), ap(rg("mbig")), ActivationFunctionType.Identity, bias=1.0, scale=-1.0 / BIG),
-       [rg("mbig")], [rg("mask")])
-    for a, b in HALVES:
-        quant("xq0", "xs0", "x0", a, b)
-
-    for t in range(R):
-        last = t == R - 1
-        X, xq, xs = "x%d" % t, "xq%d" % t, "xs%d" % t
-        X2, xq2, xs2 = "x%d" % (t + 1), "xq%d" % (t + 1), "xs%d" % (t + 1)
-        off, lr, bw = "off%d" % t, "lr%d" % t, "bw%d" % t
-        Y, yq, yp, zq, zp, kq, kp = ["%s%d" % (n, t) for n in ("yt", "yq", "yp", "zq", "zp", "kq", "kp")]
-        av, mx = "av%d" % t, "mx%d" % t
-
-        def L(k):
-            return rg(lr, 32 * k, 32 * k + 32)
-
-        for k in range(N):
-            if r in list_dsts(k):
-                lands("lst%d_%d" % (t, k), len(_list_masks(topo, cores[k], [cores[d] for d in list_dsts(k)])[core]), [L(k)])
-        ne = full(prv, r)[1]
-        if r > 0:
-            lands("dat%d_0" % t, 2 * ne, [rg(zq, 0, H), rg(zp, 0, H)])
-            lands("dat%d_1" % t, 2 * ne, [rg(zq, H, C), rg(zp, H, C)])
-        else:
-            lands("dat%d_0" % t, ne, [rg(zq, 0, H)])
-            lands("dat%d_1" % t, 2 * ne, [rg(zq, H, C), rg(zp)])
-
-        for h in range(2):
-            mm(4 + h, "uq2", "us2", 0, xq, xs, h * H, h * H + H)
-            mm(h, "uq2", "us2", 0, xq, xs, h * H, h * H + H)
-        for h in range(2):
-            copy("a", rg("sv", h * H, h * H + H), rg("ps%d" % h, 0, H))
-            tt(rg("thr", h * H, h * H + H), rg("mbig", h * H, h * H + H), rg("ps%d" % (4 + h), 0, H), SUB)
-        if t == 0:
-            copy("v", rg("pro"), rg("pri"))
-            tt(rg("dd"), rg("pri"), rg("jw"), SUB)
-        wrap(None, rg("sv"), rg("pro"), "vb", "wb", "thr", AluOpType.is_gt)
-        tt(rg("t1"), rg("wb", 15, C, 16), rg("dd"), MUL)
-        tt(rg("cw"), rg("t1"), rg("jw"), ADD)
-        copy("v", rg("o0"), rg("cw"))
-        tr(rg("asm", 64, 96), rg("cw"))
-        gather("a", rg("ta"), rg("row"), rg("o0"))
-        for a in range(3):
-            copy("v", rg("asm", 32, 64, 1, 32 * a + 32, 32 * a + 64), rg("asm", 64, 96, 1, 32 * a, 32 * a + 32))
-        copy("v", rg("asm", 0, 32, 1, 64, 128), rg("asm", 64, 96, 1, 0, 64))
-        tr(rg("bt", 0, 64), rg("asm", 16, 80))
-        tr(rg("bt", 64, 96), rg("asm", 32, 64))
-        copy("v", rg("ou"), rg("bt"))
-
-        split("tb", "ta", "ou", 32)
-        split("ta", "tb", "ou", 64)
-        gather("a", rg("tb"), rg("ta"), rg("ou", 0, 32))
-        wrap(rg("o4", 0, 32, 1, 64, 128), rg("ta"), rg("ou", 0, 32), "tm4", "ts4")
-        if last:
-            gather("a", rg("t7"), rg("tb"), rg("o4"))
-        wrap(None, rg("tb"), rg("o4"), "tm", "ts")
-
-        def offs(k, a=0, b=C):
-            ts(rg(off, 32 * k + a // 16, 32 * k + b // 16), rg("ts", a + 15, b, 16), 4.0, MUL, float(k), ADD)
-
-        dsts = list_dsts(r)
-        offs(0, 0, H)
-        offs(1, 0, H)
-        if dsts:
-            tr(rg("sa", 0, 32, 1, 96, 128), rg("ts", 15, C, 16, 96, 128))
-            offs(2)
-            offs(0, H, C)
-            copy("v", rg("sa", 0, 16, 1, 96, 128), rg("sa", 16, 32, 1, 96, 128))
-            offs(3)
-            offs(1, H, C)
-            tr(rg("sc", 0, 32, 1, 96, 128), rg("sa", 0, 32, 1, 96, 128))
-            for q in range(4):
-                copy("v", rg(lr, 32 * r, 32 * r + 32, 1, 32 * q, 32 * q + 32), rg("sc", 0, 32, 1, 96, 128))
-            em = _list_masks(topo, core, [cores[d] for d in dsts])
-            order("g", [L(r)], [])
-            trs, late = [], []
-            for d in dsts:
-                rid, pid, _ = topo.addr(cores[d])
-                x = RemoteDMATransfer(dst_ids=[DstId(rid=rid, pnc=pid)], dma_engine_mask=sum(1 << e for e in em[cores[d]]),
-                                      remote_sem=T.sem["lst%d_%d" % (t, r)], src=ap(L(r)), dst=ap(L(r)))
-                own = set(em[cores[d]]) <= set(topo.engines(core, cores[nxt]))
-                (trs if own or t > 0 else late).append(x)
-                cnt["sent"] = cnt.get("sent", 0) + len(em[cores[d]])
-            g.remote_dma_fused(trs, local_sem=T.sem.sent)
-            if late:
-                g.remote_dma_fused(late, local_sem=T.sem.sent)
-        else:
-            offs(2)
-            offs(3)
-            offs(0, H, C)
-            offs(1, H, C)
-
-        rid, pid, _ = topo.addr(cores[nxt])
-        msk, ne = full(r, nxt)
-
-        def send(out, in_, h):
-            g.remote_dma(out, in_, T.sem["dat%d_%d" % (t, h)], T.sem.sent, pid, rid, msk)
-            cnt["sent"] = cnt.get("sent", 0) + ne
-
-        def ypart(q, k, a, b):
-            gather(q, rg(Y, 4 * a + k, 4 * b, 4), rg(X), rg(off, 32 * k + a // 16, 32 * k + b // 16))
-
-        for h, (a, b) in enumerate(HALVES):
-            mid = (a + b) // 2
-            ypart("a", 0, a, b)
-            ypart("a", 1, a, b)
-            if h == 0:
-                ypart("a" if dsts else "v", 2, a, b)
-                ypart("v", 3, a, b)
-            else:
-                ypart("a", 2, a, mid)
-                ypart("v", 3, a, b)
-                ypart("v", 2, mid, b)
-            quant(yq, yp, Y, a, b)
-            order("g", [rg(yq, a, b)], [])
-            send(ap(rg(zq, a, b)).bitcast(dt.uint8), ap(rg(yq, a, b)).bitcast(dt.uint8), h)
-            if nxt > 0:
-                send(ap(rg(zp, a, b)), ap(rg(yp, a, b)), h)
-            elif h == 1:
-                send(ap(rg(zp)), ap(rg(yp)), h)
-
-        def pick(iq, ip, lst, a, b):
-            o = rg(lst[0], lst[3] + a // 16, lst[3] + b // 16)
-            pick_codes(rg(kq, a, b), rg(iq), o)
-            gather("a", rg(kp, a, b), rg(ip), o)
-
-        def vmax(b, h):
-            tt(rg(mx, C * b + h * H, C * b + h * H + H), rg("ps%d" % (4 + b), 0, H), rg(av, C * b + h * H, C * b + h * H + H), AluOpType.max)
-
-        def xcols(b, h):
-            return rg(X2, 4 * h * H + b, 4 * (h * H + H), 4)
-
-        def plain(b, h):
-            copy("a", xcols(b, h), rg(mx, C * b + h * H, C * b + h * H + H), SC)
-
-        def undo(q, b, h):
-            gather(q, xcols(b, h), rg(mx, C * b, C * b + C), rg(back[0], back[3] + 16 * h, back[3] + 16 * h + 16), SC)
-
-        todo = [(b, h) for h in range(2) for b in range(4)]
-
-        def vcopy(n):
-            while len(todo) > 8 - n:
-                b, h = todo.pop(0)
-                src = rg("ps%d" % b, h * H, h * H + H) if r == 0 else rg("ps%d" % (b + 4 - 4 * h), 0, H)
-                copy("a", rg(av, C * b + h * H, C * b + h * H + H), src)
-
-        back = None
-        if r == 0:
-            for b in range(4):
-                mm(b, "vq", "vp", 128 * b, yq, yp, 0, C)
-            if last:
-                dma("s", "outs", T.ol[:, :], T.t7[0:128:16, :], [rg("t7")], [])
-            else:
-                vcopy(2)
-                quant("aq", "asc", "ab", 0, 128)
-            split("la", "row", lr, 64)
-            split("lb", "la", lr, 32)
-            vcopy(6)
-            wrap(rg(bw), rg("lb"), L(0), "tm2", "ts2")
-            for a, b in HALVES:
-                pick(zq, zp, rg(bw), a, b)
-            vcopy(8)
-            wq_, wp_ = kq, kp
-        else:
-            if t == 0:
-                quant("aq", "asc", "ab", 0, 128)
-            if r == 3 and last:
-                split("la", "row", lr, 32)
-            pick(yq, yp, L(r - 1), 0, H)
-            for b in range(4):
-                mm(4 + b, "vq", "vp", 128 * b, kq, kp, 0, H)
-            pick(yq, yp, L(r - 1), H, C)
-            if r == 3 and not last:
-                split("la", "row", lr, 32)
-            for b in range(4):
-                mm(b, "vq", "vp", 128 * b, kq, kp, H, C)
-            wq_, wp_ = zq, zp
-            if r == 1:
-                if last:
-                    gather("v", rg("t8"), rg("t7"), L(0))
-                    dma("s", "outs", T.ol[:, :], T.t8[0:128:16, :], [rg("t8")], [])
-            elif r == 2:
-                back = L(0)
-                if last:
-                    gather("v", rg("t8"), rg("t7"), L(1))
-            else:
-                wrap(rg(bw), rg("la"), L(0), "tm2", "ts2")
-                back = rg(bw)
-            vcopy(8)
-
-        for b in range(4):
-            mm(4 + b, "wq", "wp", 128 * b, wq_, wp_, 0, H)
-        for b in range(4):
-            vmax(b, 0)
-            mm(4 + b, "wq", "wp", 128 * b, wq_, wp_, H, C)
-            if back is None:
-                plain(b, 0)
-        for b in range(4):
-            vmax(b, 1)
-            if back is None:
-                plain(b, 1)
-        if back is None:
-            quant(xq2, xs2, X2, 0, H)
-            quant(xq2, xs2, X2, H, C)
-        else:
-            for b, h in ((0, 0), (1, 0), (2, 0), (0, 1), (1, 1)):
-                undo("a", b, h)
-            undo("v", 3, 0)
-            undo("v", 3, 1)
-            quant(xq2, xs2, X2, 0, H)
-            undo("v", 2, 1)
-            quant(xq2, xs2, X2, H, C)
-
-    xq, xs = "xq%d" % R, "xs%d" % R
-    if r == N - 1:
-        gather("a", rg("t8"), rg("t7"), rg("lr%d" % (R - 1), 64, 96))
-    if r == 2:
-        gather("a", rg("t9"), rg("t8"), rg("lr%d" % (R - 1), 0, 32))
-        dma("a", "outs", T.ol[:, :], T.t9[0:128:16, :], [rg("t9")], [])
-    for h in range(2):
-        mm(4 * h, "aq", "asc", 0, xq, xs, h * H, h * H + H)
-        dma("s", "outs", T.oc[:, 4 * h * H:4 * (h * H + H)], ap(rg(xq, h * H, h * H + H)).bitcast(dt.uint8), [rg(xq, h * H, h * H + H)], [])
-    for k in range(4):
-        dma("s", "outs", T.osc[4 * k:4 * k + 4, :], T[xs][32 * k:32 * k + 4, :], [rg(xs)], [])
-    for h in range(2):
-        copy("a" if h == 0 and r < 2 else "v", rg("ysb", h * H, h * H + H), rg("ps%d" % (4 * h), 0, H))
-        dma("s" if r >= 2 else "a", "outs", T.y[:, h * H:h * H + H], ap(rg("ysb", h * H, h * H + H)), [rg("ysb", h * H, h * H + H)], [])
-    if r == N - 1:
-        split("t9", "t8", "bw%d" % (R - 1), 0)
-        dma("a", "outs", T.ol[:, :], T.t9[0:128:16, :], [rg("t9")], [])
+    byname = {c[0]: c for c in calls}
+    for name, q in merge(calls, ORDER[r]):
+        _, qs, kind, fn, reads, writes = byname[name]
+        assert q in qs
+        order(q, reads, writes)
+        if kind[0] == "far":
+            fn(q)
+            cnt["sent"] = cnt.get("sent", 0) + kind[1]
+            continue
+        sem, n = (CS[q], 1) if kind == "op" else (kind[1], 16)
+        fn(q).then_inc(T.sem[sem], n)
+        cnt[sem] = cnt.get(sem, 0) + n
+        note(q, (sem, cnt[sem], dict(known[q])), reads, writes)
 
     for sem in sorted(cnt, key=lambda k: k == "outs"):
         if waited.get(sem, 0) < cnt[sem]:

from concourse.bass import DstId, RemoteDMATransfer
from concourse.mybir import dt, AluOpType, ActivationFunctionType

C = 512
R = 2
H = C // 2
SC = 0.03125
MID = 256.0
UP, DOWN = 4096.0, -1024.0
X4 = "float8_e4m3fn_x4"

PAR = {
    "xcut": [[(0, 256, 384, 512)] * 3] * 4,
    "ycut": [(0, 256, 512)] * 4,
    "whole": [False, False, False, True],
    "lists": [[[1, 2, 3]], [[2, 3, 0]], [[3, 0]], []],
    "kcut": (0, 256, 512),
    "pcut": (0, 256, 512),
    "fcut": (0, 256, 384, 512),
    "vcut": (0, 256, 512),
    "wcut": (0, 128, 320, 512),
    "bcut": (0, 128, 320, 512),
    "yshare": 18,
}

ORDER = {
    0: {
        "v": "pi2 pi0 pi1 pf jw fx0 ka16 uoff fx1 id0 qu kb16 puc o4i qx0 wz qx1 e0 kk16 fx3 qx2 dd pro fd jw2 vb0.0 vb1.0 wb0.0 wb1.0 id1 cw.0 tn0.0 o0.0 tn1.0 tn2.0 tm.0 to.0 b2.0 b1.0 b3.0 ou1.0 ou2.0 g20.0 g30.0 g40.0 g42.0 s10.0 s11.0 s12.0 o40.0 o41.0 o42.0 g50.0 g52.0 s40.0 s41.0 s42.0 la.0 of2.0 lb.0 of0.0 lc3.0 lc2.0 of3.0 lr1.0 lr0.0 of1.0 qa y11.0 y10.0 qy0.0 qy1.0 av02.0 av10.0 La0.0 Lb1.0 Lc2.0 Lc0.0 s21.0 s20.0 s22.0 bw1.0 bw0.0 bw2.0 pk0c.0 pk1c.0 mx00.0 mx02.0 mx03.0 mx01.0 mx13.0 mx12.0 mx10.0 mx11.0 x10.0 qn0.0 x20.0 qn1.0 qn2.0 nv0.1 sv1.1 vb0.1 vb1.1 wb0.1 wb1.1 cw.1 tn0.1 o0.1 tm.1 tn2.1 tn1.1 to.1 b1.1 b3.1 b2.1 ou1.1 ou2.1 g20.1 g30.1 g42.1 s10.1 s12.1 s11.1 o40.1 o42.1 o41.1 g52.1 s40.1 s42.1 s41.1 la.1 of3.1 of2.1 lb.1 of1.1 of0.1 lc3.1 lc2.1 y00.1 lr1.1 lr0.1 y11.1 y13.1 qy0.1 La0.1 qy1.1 Lb0.1 av03.1 Lc1.1 av02.1 s21.1 s20.1 s22.1 bw1.1 bw0.1 bw2.1 pk0c.1 pk1c.1 mx00.1 mx02.1 mx03.1 mx01.1 mx13.1 mx10.1 mx11.1 mx12.1 qn0.1 x10.1 qn2.1 qn1.1 ys0",
        "a": "lu pg fx2 pup sv0.0 nv0.0 sv1.0 sv2.0 nv1.0 nv2.0 g10.0 g21.0 g31.0 g41.0 g51.0 y12.0 y02.0 y13.0 y03.0 y01.0 y00.0 av01.0 La1.0 Lb0.0 Lc1.0 av03.0 av00.0 pk0p.0 av11.0 pk1p.0 av13.0 av12.0 x01.0 x00.0 x11.0 x21.0 sv0.1 sv2.1 nv1.1 nv2.1 g10.1 g21.1 g31.1 g40.1 g41.1 g50.1 g51.1 y03.1 y02.1 y01.1 y12.1 y10.1 La1.1 Lb1.1 av00.1 Lc0.1 Lc2.1 av13.1 av01.1 pk0p.1 av10.1 pk1p.1 ol av11.1 av12.1 x00.1 x01.1 x21.1 x20.1 x11.1 ys2 dy0 dy2 ys1 ds1",
        "p": "ms0.0 mt0.0 ms1.0 ms2.0 mt1.0 mt2.0 mv02.0 mv10.0 mv01.0 mv00.0 mv03.0 mv11.0 mv13.0 mv12.0 mw00.0 mw02.0 mw03.0 mw01.0 mw10.0 mw13.0 mw12.0 mw11.0 ms0.1 mt0.1 ms1.1 ms2.1 mt1.1 mt2.1 mv02.1 mv00.1 mv03.1 mv11.1 mv13.1 mv01.1 mv12.1 mv10.1 mw00.1 mw02.1 mw01.1 mw03.1 mw10.1 mw13.1 mw11.1 mw12.1 my0 my2 my1",
        "s": "lx0 lx1 lx2 lp lvq lvp lwq lwp lab dl dc0 dc2 dc1 ds2 ds3 ds0 dy1",
        "g": "ipcol ik16 ijm16 ik4 irow sl0.0 sq0.0 sp0.0 sq1.0 sp1.0 sl0.1 sq0.1 sp0.1 sq1.1 sp1.1",
    },
    1: {
        "v": "pi2 pi1 pi0 pf uoff pg fx0 jw ka16 qu kb16 puc id1 qx0 kk16 qx1 fx3 id0 qx2 dd wz pro fd sv2.0 jw2 vb0.0 vb1.0 wb0.0 wb1.0 cw.0 o0.0 tn1.0 tm.0 tn0.0 tn2.0 to.0 b1.0 b3.0 b2.0 ou1.0 ou2.0 g20.0 g30.0 g41.0 o4i s11.0 s12.0 o41.0 s10.0 o42.0 o40.0 g52.0 s41.0 s42.0 s40.0 la.0 of2.0 lb.0 of3.0 lc2.0 lc3.0 of1.0 lr1.0 lr0.0 qa of0.0 y02.0 y03.0 y11.0 qy0.0 qy1.0 pk0c.0 pk1c.0 av00.0 av03.0 av12.0 mx00.0 mx01.0 mx02.0 mx03.0 mx10.0 mx12.0 mx13.0 mx11.0 qn0.0 x20.0 x21.0 qn1.0 qn2.0 sv0.1 nv1.1 nv2.1 vb0.1 vb1.1 wb0.1 wb1.1 cw.1 tm.1 o0.1 tn0.1 tn2.1 tn1.1 to.1 b1.1 b2.1 ou1.1 b3.1 g21.1 ou2.1 g31.1 g40.1 s10.1 s11.1 o40.1 s12.1 o41.1 o42.1 g51.1 s40.1 s41.1 s42.1 la.1 of3.1 lb.1 of1.1 lc3.1 lc2.1 of2.1 of0.1 lr1.1 lr0.1 y02.1 qy0.1 y12.1 y11.1 qy1.1 pk0c.1 pk1p.1 pk1c.1 av03.1 av02.1 mx00.1 mx03.1 av13.1 mx01.1 mx02.1 mx11.1 mx12.1 mx13.1 mx10.1 x20.1 x10.1 qn2.1 qn0.1 qn1.1 ys0 ys1",
        "a": "lu fx1 e0 fx2 pup sv0.0 nv0.0 sv1.0 nv1.0 nv2.0 g10.0 g21.0 g31.0 g42.0 g40.0 g51.0 g50.0 y12.0 y13.0 y00.0 y01.0 y10.0 pk0p.0 pk1p.0 av01.0 av02.0 av10.0 av13.0 av11.0 x00.0 x01.0 x10.0 x11.0 nv0.1 sv1.1 sv2.1 g10.1 g20.1 g30.1 g41.1 g42.1 g50.1 g52.1 y03.1 y01.1 y00.1 y10.1 y13.1 pk0p.1 ol1 ol0 av00.1 av01.1 av11.1 av10.1 av12.1 x00.1 x01.1 x21.1 x11.1 dl dc0 ys2 dy2 dy1",
        "p": "ms0.0 mt0.0 ms1.0 ms2.0 mt1.0 mt2.0 mv00.0 mv01.0 mv03.0 mv02.0 mv10.0 mv12.0 mw00.0 mw01.0 mw02.0 mv13.0 mw03.0 mv11.0 mw10.0 mw12.0 mw13.0 mw11.0 mt0.1 ms0.1 ms1.1 mt1.1 ms2.1 mt2.1 mv03.1 mv02.1 mv00.1 mv13.1 mv10.1 mv01.1 mv11.1 mw00.1 mw03.1 mv12.1 mw01.1 mw02.1 mw11.1 mw10.1 mw12.1 mw13.1 my2 my0 my1",
        "s": "lx0 lx1 lx2 lp lvq lvp lwq lwp lab dc2 ds1 dc1 ds2 ds3 ds0 dy0",
        "g": "ipcol ik16 ijm16 ik4 irow sl0.0 sq0.0 sp0.0 sq1.0 sp1.0 sl0.1 sq0.1 sp0.1 sq1.1 sp1.1",
    },
    2: {
        "v": "pi0 pi1 pi2 pf fx0 pg jw uoff ka16 qu kb16 puc id1 o4i qx0 kk16 qx1 wz fx3 qx2 dd pro fd sv2.0 jw2 vb0.0 vb1.0 wb0.0 wb1.0 cw.0 id0 o0.0 tn1.0 tn2.0 tm.0 tn0.0 to.0 b1.0 b2.0 b3.0 ou1.0 ou2.0 g20.0 g30.0 qa g42.0 s10.0 s12.0 s11.0 o40.0 o42.0 o41.0 g52.0 s40.0 s42.0 s41.0 la.0 lb.0 lc3.0 lc2.0 of2.0 lr0.0 lr1.0 y12.0 of3.0 of0.0 y13.0 y00.0 of1.0 y02.0 qy0.0 qy1.0 pk0c.0 pk1c.0 av03.0 av01.0 mx00.0 mx01.0 mx03.0 mx02.0 mx10.0 mx11.0 mx13.0 mx12.0 x03.0 x02.0 x12.0 qn0.0 x22.0 qn1.0 qn2.0 sv0.1 sv2.1 vb0.1 vb1.1 wb0.1 wb1.1 cw.1 o0.1 tm.1 tn1.1 tn2.1 tn0.1 to.1 b1.1 b2.1 b3.1 ou1.1 ou2.1 g20.1 g30.1 g40.1 g42.1 s10.1 s11.1 s12.1 o40.1 o41.1 o42.1 g51.1 s40.1 s41.1 s42.1 la.1 of0.1 lb.1 of3.1 of2.1 lc2.1 lc3.1 of1.1 lr1.1 lr0.1 y03.1 y11.1 qy0.1 y12.1 qy1.1 pk0c.1 pk1c.1 av01.1 av00.1 av02.1 av11.1 mx01.1 mx00.1 mx02.1 mx03.1 mx10.1 mx11.1 mx12.1 mx13.1 x10.1 qn1.1 qn0.1 qn2.1 pf2c pf1c pf0c pf2p ys1 ys0",
        "a": "lu fx1 fx2 pup sv0.0 nv0.0 e0 sv1.0 nv2.0 nv1.0 g10.0 g21.0 g31.0 g40.0 g41.0 g50.0 g51.0 y03.0 y01.0 y11.0 y10.0 pk0p.0 pk1p.0 av00.0 av10.0 av02.0 av13.0 av11.0 av12.0 x20.0 x00.0 x01.0 x10.0 x11.0 x21.0 x13.0 x23.0 nv0.1 sv1.1 nv1.1 nv2.1 g10.1 g21.1 g31.1 g41.1 g50.1 g52.1 y00.1 y02.1 y01.1 y13.1 y10.1 ok1 pk0p.1 pk1p.1 ok0 av03.1 av10.1 ol1 av12.1 av13.1 x00.1 x01.1 x11.1 x21.1 x20.1 ol0 pf1p pf0p dc1 dc0 ys2",
        "p": "ms0.0 mt0.0 ms1.0 ms2.0 mt2.0 mt1.0 mv03.0 mv00.0 mv01.0 mv10.0 mv02.0 mv13.0 mw03.0 mw00.0 mw01.0 mv11.0 mv12.0 mw02.0 mw10.0 mw11.0 mw12.0 mw13.0 ms0.1 mt0.1 ms1.1 ms2.1 mt1.1 mt2.1 mv01.1 mv00.1 mv03.1 mv02.1 mv11.1 mv10.1 mw01.1 mw00.1 mv12.1 mw02.1 mw03.1 mv13.1 mw10.1 mw11.1 mw12.1 mw13.1 my1 my0 my2",
        "s": "lx0 lx1 lx2 lp lvq lvp lwq lwp lab dl dc2 ds3 dy1 ds2 ds0 ds1 dy0 dy2",
        "g": "ipcol ik4 ik16 ijm16 irow sl0.0 sq0.0 sp0.0 sq1.0 sp1.0 sl0.1 sq0.1 sp0.1 sq1.1 sp1.1",
    },
    3: {
        "v": "pi0 pi1 pi2 pf ka16 fx0 uoff jw kb16 id0 qu wz fx2 puc id1 kk16 qx0 kb4 qx1 ka4 qx2 o4i dd nv0.0 fd nv1.0 pro jw2 nv2.0 vb0.0 vb1.0 wb0.0 wb1.0 cw.0 tn0.0 o0.0 to.0 tn1.0 tm.0 tn2.0 b1.0 b3.0 b2.0 ou1.0 ou2.0 g21.0 g31.0 g42.0 fx3 kk4 s11.0 s10.0 o41.0 s12.0 o40.0 o42.0 g52.0 s40.0 s41.0 of0.0 of1.0 y00.0 s42.0 qy0.0 of2.0 y11.0 qy1.0 qa pk0c.0 pk1c.0 La0.0 La1.0 av03.0 mx01.0 mx00.0 mx03.0 mx02.0 s20.0 mx12.0 mx10.0 mx11.0 s21.0 mx13.0 bw.0 x03.0 x01.0 x21.0 qn0.0 x20.0 qn1.0 qn2.0 sv2.1 vb0.1 vb1.1 wb0.1 wb1.1 cw.1 o0.1 tn2.1 tn0.1 tn1.1 tm.1 to.1 b1.1 b3.1 b2.1 ou1.1 ou2.1 g21.1 g31.1 g41.1 s10.1 s11.1 o40.1 s12.1 o41.1 o42.1 g51.1 s40.1 s41.1 of0.1 of1.1 s42.1 y00.1 of2.1 qy0.1 y11.1 qy1.1 La0.1 pk0c.1 pk1c.1 ok1 Lb0.1 av03.1 av02.1 mx00.1 mx01.1 mx02.1 mx03.1 mx11.1 mx10.1 mx12.1 mx13.1 s20.1 s21.1 x21.1 bw.1 qn0.1 qn2.1 qn1.1 pf1c pf0c pf2c pf2p ys1 ys0",
        "a": "lu pg e0 pup sv0.0 fx1 sv2.0 sv1.0 g10.0 g20.0 g30.0 g41.0 g40.0 g51.0 g50.0 y01.0 y10.0 pk0p.0 pk1p.0 av01.0 av00.0 av02.0 av12.0 Lb0.0 av10.0 av11.0 av13.0 Lb1.0 x02.0 x00.0 x10.0 x11.0 sv0.1 nv0.1 sv1.1 nv1.1 nv2.1 g10.1 g20.1 g30.1 g40.1 g42.1 g50.1 g52.1 y01.1 y10.1 La1.1 pk0p.1 pk1p.1 ok0 av00.1 av01.1 Lb1.1 av11.1 av12.1 av10.1 av13.1 x01.1 x00.1 x20.1 x11.1 x10.1 ol0 pf1p pf0p ol1 ds2 dy1 ys2 dy0 ds1",
        "p": "mt0.0 ms0.0 ms1.0 mt1.0 ms2.0 mt2.0 mv01.0 mv00.0 mv02.0 mv03.0 mv12.0 mv10.0 mw01.0 mw00.0 mw03.0 mw02.0 mv11.0 mw12.0 mv13.0 mw10.0 mw11.0 mw13.0 ms0.1 mt0.1 ms1.1 ms2.1 mt2.1 mt1.1 mv00.1 mv02.1 mv01.1 mv03.1 mv11.1 mv12.1 mw00.1 mw01.1 mv10.1 mv13.1 mw02.1 mw03.1 mw11.1 mw10.1 mw12.1 mw13.1 my1 my0 my2",
        "s": "lx0 lx1 lx2 lp lvq lvp lwq lwp lab dc1 dc0 dc2 dl ds3 ds0 dy2",
        "g": "ipcol ijm16 ik16 ijm4 irow sq0.0 sq1.0 sp1.0 sq0.1 sq1.1 sp1.1",
    },
}


def _scratch():
    s = {}

    def sb(n, w, d):
        s[n] = ("sbuf", [128, w], d)
    for n in ("ub", "ab"):
        sb(n, 512, "bfloat16")
    for n in ("uq", "uq2", "aq"):
        sb(n, 128, X4)
    for n in ("us", "us2", "asc"):
        sb(n, 128, "uint8")
    for n in ("vq", "wq", "fq"):
        sb(n, C, X4)
    for n in ("vp", "wp", "fp"):
        sb(n, C, "uint8")
    sb("pri", 32, "int32"); sb("pro", 32, "uint16"); sb("e3", 96, "float32"); sb("fd", 32, "float32")
    sb("pcol", 2, "int32"); sb("pi", 4, "int32"); sb("pf", 4, "float32"); sb("pg", 2, "float32"); sb("fx", 4, "float32")
    sb("k4", 4, "float32"); sb("f4", 4, "float32"); sb("k16", 32, "float32"); sb("jw", 32, "float32"); sb("uoff", 8, "uint16")
    for n in ("jm16", "jm4", "ka16", "kb16", "ka4", "kb4", "kk16", "kk4"):
        sb(n, H, "bfloat16")
    sb("sv", C, "float32"); sb("nv", C, "float32"); sb("vb", C, "bfloat16")
    sb("wb", 3 * C, "float16"); sb("cw", 96, "float32"); sb("o0", 32, "uint16"); sb("o4", 32, "uint16")
    sb("asm", 96, "float32"); sb("bt", 96, "float32"); sb("ou", 96, "uint16")
    for n in ("row", "r1", "r2", "r3", "r4", "r5", "la", "lb", "lc", "t8"):
        sb(n, C, "bfloat16")
    for n in ("t9", "ysb"):
        sb(n, C, "float32")
    for n in ("s1", "s4", "s2"):
        sb(n, C, "float16")
    sb("sa", 32, "float16"); sb("sc", 32, "float16")
    for t in range(R + 1):
        sb("x%d" % t, 4 * C, "bfloat16"); sb("xq%d" % t, C, X4); sb("xs%d" % t, C, "uint8")
    for t in range(R):
        sb("off%d" % t, 128, "uint16"); sb("lr%d" % t, 96, "uint16"); sb("bw%d" % t, 128, "uint16")
        sb("yt%d" % t, 4 * C, "bfloat16")
        for n in ("y", "z", "k"):
            sb("%sq%d" % (n, t), C, X4); sb("%sp%d" % (n, t), C, "uint8")
        sb("av%d" % t, 4 * C, "float32"); sb("mx%d" % t, 4 * C, "float32")
    for b in range(8):
        s["ps%d" % b] = ("psum", [128, 512], "float32")
    return s


SCRATCH = _scratch()
SEMAPHORES = (["cv", "ca", "cp", "cg", "sent", "outs"] + ["ld%d" % i for i in range(12)]
              + ["lst%d_%d" % (t, k) for t in range(R) for k in range(3)] + ["dat%d_%d" % (t, h) for t in range(R) for h in range(4)])


def _list_masks(topo, src, dsts, busy):
    eng = {d: topo.engines(src, d) for d in dsts}
    few = min(len(e) for e in eng.values())
    narrow = [d for d in dsts if len(eng[d]) == few]
    used, out = set(), {}
    for d in narrow + [d for d in dsts if d not in narrow]:
        free = [e for e in eng[d] if e not in used][::-1]
        want = few // len(narrow) if d in narrow else len(free)
        n = 1
        while 2 * n <= min(want, len(free), busy):
            n *= 2
        used.update(free[:n])
        out[d] = free[:n]
    return out


def rg(name, c0=0, c1=None, step=1, p0=0, p1=128):
    return (name, p0, p1, c0, SCRATCH[name][1][1] if c1 is None else c1, step)


def meet(x, y):
    if x[0] != y[0]:
        return False
    if x[0].startswith("ps"):
        return True
    if x[2] <= y[1] or y[2] <= x[1] or x[4] <= y[3] or y[4] <= x[3]:
        return False
    if x[5] == 1 and y[5] == 1:
        return True
    return bool(set(range(x[3], x[4], x[5])) & set(range(y[3], y[4], y[5])))


def runs(cut):
    return list(zip(cut, cut[1:]))


def parts(a, b, n):
    return runs([a + (b - a) * i // n for i in range(n + 1)])


def plan(g, core, T, topo):
    r = T.rank_of(core)
    cores = T.cores
    N = len(cores)
    Q = {"v": g.vector, "a": g.scalar, "p": g.tensor, "s": g.sync, "g": g}
    ADD, MUL, SUB, MIN = AluOpType.add, AluOpType.mult, AluOpType.subtract, AluOpType.min
    COPY, IDENT = ActivationFunctionType.Copy, ActivationFunctionType.Identity
    HALVES = ((0, H), (H, C))
    calls, lands, tag = [], [], [""]

    def ap(x):
        n, p0, p1, c0, c1, st = x
        return T[n][p0:p1, c0:c1] if st == 1 else T[n][p0:p1, c0:c1:st]

    def op(name, qs, fn, reads, writes, kind="op"):
        calls.append((name + tag[0], qs, kind, fn, reads, writes))

    def dma(name, qs, sem, out, in_, reads, writes):
        op(name, qs, lambda q: Q[q].dma_start(out, in_), reads, writes, ("dma", sem))

    def move(name, qs, out, in_, off=None, mul=None, add=None):
        def fn(q):
            i = ap(in_) if off is None else ap(in_).indirect(ap(off))
            if q == "a":
                if add is not None:
                    return g.scalar.activation(ap(out), i, IDENT, bias=add)
                if mul is not None:
                    return g.scalar.activation(ap(out), i, COPY, scale=mul)
                return g.scalar.activation(ap(out), i, COPY)
            if add is not None:
                return g.vector.tensor_scalar(ap(out), i, add, None, ADD)
            if mul is not None:
                return g.vector.tensor_scalar(ap(out), i, mul, None, MUL)
            return g.vector.tensor_copy(ap(out), i)
        op(name, qs, fn, [in_] + ([] if off is None else [off]), [out])

    def sub(lst, a, b):
        return rg(lst[0], lst[3] + a // 16, lst[3] + b // 16)

    def compose(name, out, win, lst, cut=HALVES, add=None):
        for i, (a, b) in enumerate(cut):
            move("%s%d" % (name, i), "av", rg(out, a, b), rg(win), sub(lst, a, b), add=add)

    def tt(name, out, a, b, alu, off=None):
        if off is None:
            op(name, "v", lambda q: g.vector.tensor_tensor(ap(out), ap(a), ap(b), alu), [a, b], [out])
        else:
            op(name, "v", lambda q: g.vector.tensor_tensor(ap(out), ap(a).indirect(ap(off)), ap(b), alu), [a, b, off], [out])

    def ts(name, out, a, s1, op0, s2=None, op1=None):
        col = [s for s in (s1, s2) if isinstance(s, tuple)]
        v1, v2 = [ap(s) if isinstance(s, tuple) else s for s in (s1, s2)]
        if op1 is None:
            op(name, "v", lambda q: g.vector.tensor_scalar(ap(out), ap(a), v1, None, op0), [a] + col, [out])
        else:
            op(name, "v", lambda q: g.vector.tensor_scalar(ap(out), ap(a), v1, v2, op0, op1), [a] + col, [out])

    def tr(name, out, in_):
        op(name, "v", lambda q: g.vector.transpose(ap(out), ap(in_)), [in_], [out])

    def scan(name, out, d0, d1, op0, op1):
        op(name, "v", lambda q: g.vector.tensor_tensor_scan(ap(out), ap(d0), ap(d1), 0.0, op0, op1), [d0, d1], [out])

    def wrap(name, out, row, steps, cut, p1=128, step=1):
        for i, (a, b) in enumerate(cut):
            scan("%s%d" % (name, i), rg(out, step * a, step * b, step, 0, p1), rg(steps, 0, b - a, 1, 0, p1), rg(row, a, b, 1, 0, p1), ADD, MIN)

    def quant(name, q_, s, tile, a, b):
        o1, o2, i = rg(q_, a, b), rg(s, a, b), rg(tile, 4 * a, 4 * b)
        op(name, "v", lambda q: g.vector.quantize_mx(ap(o1), ap(o2), ap(i)), [i], [o1, o2])

    def mm(name, bank, wq, ws, w0, xq, xs, a, b):
        o, i = rg("ps%d" % bank, 0, b - a), [rg(wq, w0, w0 + 128), rg(ws, w0, w0 + 128), rg(xq, a, b), rg(xs, a, b)]
        op(name, "p", lambda q: g.tensor.matmul_mx(ap(o), ap(i[0]), ap(i[1]), ap(i[2]), ap(i[3]), True, True), i, [o])

    def pick(name, oq, op_, iq, ip, off):
        op(name + "c", "v", lambda q: g.vector.tensor_copy(ap(oq).bitcast(dt.uint32), ap(iq).bitcast(dt.uint32).indirect(ap(off))), [iq, off], [oq])
        move(name + "p", "av", op_, ip, off)

    def iota(name, pattern, base, cm, flt):
        out = rg(name)
        if flt:
            op("i" + name, "g", lambda q: g.iota(ap(out), pattern, base, cm, allow_small_or_imprecise_dtypes=True), [], [out])
        else:
            op("i" + name, "g", lambda q: g.iota(ap(out), pattern, base, cm), [], [out])

    def col(name, j, p0=0, p1=128):
        return rg(name, j, j + 1, 1, p0, p1)

    def full(src, dst):
        return topo.mask(cores[src], cores[dst]), len(topo.engines(cores[src], cores[dst]))

    def list_engines(k, dsts):
        return _list_masks(topo, cores[k], [cores[d] for d in dsts], min(full(i, (i + 1) % N)[1] for i in range(N)))

    nxt, prv = (r + 1) % N, (r - 1) % N
    xcut = PAR["xcut"][r]
    four = r == N - 1

    dma("lu", "as", "ld1", ap(rg("ub")), T.u[:, :], [], [rg("ub")])
    for i, (a, b) in enumerate(runs(xcut[0])):
        dma("lx%d" % i, "sa", "ld%d" % (8 + i), ap(rg("x0", 4 * a, 4 * b)), T.x[:, 4 * a:4 * b], [], [rg("x0", 4 * a, 4 * b)])
    dma("lp", "as", "ld0", ap(rg("pri")), T.pr[:, :], [], [rg("pri")])
    dma("lvq", "s", "ld4", ap(rg("vq")).bitcast(dt.uint8), T.vc[:, :], [rg("x0")], [rg("vq")])
    dma("lvp", "s", "ld5", ap(rg("vp")), T.vs[:, :], [rg("x0")], [rg("vp")])
    dma("lwq", "s", "ld6", ap(rg("wq")).bitcast(dt.uint8), T.wc[:, :], [rg("x0")], [rg("wq")])
    dma("lwp", "s", "ld7", ap(rg("wp")), T.ws[:, :], [rg("x0")], [rg("wp")])
    dma("lab", "s", "ld2", ap(rg("ab")), T.a[:, :], [rg("x0")], [rg("ab")])

    iota("k16", [[16, 32]], 0, 0, True)
    iota("pcol", [[0, 2]], 0, 1, False)
    iota("jm16", [[0, H // 16], [1, 16]], 0, 0, True)
    iota("row", [[1, C]], -int(MID), 0, True)
    if four:
        iota("jm4", [[0, H // 4], [1, 4]], 0, 0, True)
    else:
        iota("k4", [[1, 4]], 0, 0, True)
    move("uoff", "v", rg("uoff"), rg("k16", 0, 8))
    ts("pi0", col("pi", 0), col("pcol", 0), 15, AluOpType.bitwise_and)
    ts("pi1", col("pi", 1), col("pcol", 0), 2, AluOpType.arith_shift_right, 3, AluOpType.bitwise_and)
    ts("pi2", col("pi", 2), col("pcol", 0), 3, AluOpType.bitwise_and)
    move("pf", "v", rg("pf", 0, 3), rg("pi", 0, 3))
    move("pg", "va", rg("pg"), rg("pf", 0, 2), add=1.0)
    ts("fx0", col("fx", 0), col("pf", 0), 15.0, AluOpType.is_lt, -DOWN, MUL)
    move("fx1", "va", col("fx", 1), col("fx", 0), add=MID)
    if four:
        ts("fx2", col("fx", 2), col("pf", 1), 3.0, AluOpType.is_lt, -4.0 * DOWN, MUL)
        ts("fx3", col("fx", 3), col("fx", 2), col("pf", 2), ADD, 4.0 * MID, ADD)
    else:
        move("fx2", "va", col("fx", 2), col("fx", 1), mul=4.0)
        ts("fx3", rg("f4"), rg("k4"), col("fx", 2), ADD)
    ts("jw", rg("jw"), rg("k16"), col("pf", 0), ADD)
    for k in range(2):
        tr("id%d" % k, rg("asm", 32 * k, 32 * k + 32), rg("jw"))
    move("o4i", "v", rg("o4", 0, 32, 1, 0, 64), rg("jw", 0, 32, 1, 0, 64))
    for j, n in enumerate(("16", "4") if four else ("16",)):
        ts("ka" + n, rg("ka" + n), rg("jm" + n), col("pf", j), AluOpType.is_equal, UP, MUL)
        ts("kb" + n, rg("kb" + n), rg("jm" + n), col("pg", j), AluOpType.is_equal, DOWN / UP, MUL)
        scan("kk" + n, rg("kk" + n), rg("kb" + n), rg("ka" + n), MUL, ADD)
    quant("qu", "uq", "us", "ub", 0, 128)
    pick("pu", rg("uq2"), rg("us2"), rg("uq"), rg("us"), rg("uoff"))
    move("pro", "v", rg("pro"), rg("pri"))
    move("e0", "va", rg("e3", 0, 96, 3), rg("jw"))
    ts("wz", rg("wb", 13, 3 * C, 16), rg("jm16", 0, 96), 0.0, MUL)
    tt("dd", rg("e3", 1, 96, 3), rg("pri"), rg("jw"), SUB)
    ts("fd", rg("fd"), rg("e3", 1, 96, 3), col("fx", 0), MUL)
    tt("jw2", rg("e3", 2, 96, 3), rg("fd"), rg("jw"), ADD)
    for i, (a, b) in enumerate(runs(xcut[0])):
        quant("qx%d" % i, "xq0", "xs0", "x0", a, b)
    quant("qa", "aq", "asc", "ab", 0, 128)

    for t in range(R):
        tag[0] = "." + str(t)
        last = t == R - 1
        X, xq, xs = "x%d" % t, "xq%d" % t, "xs%d" % t
        X2, xq2, xs2 = "x%d" % (t + 1), "xq%d" % (t + 1), "xs%d" % (t + 1)
        off, lr, bw = "off%d" % t, "lr%d" % t, "bw%d" % t
        Y, yq, yp, zq, zp, kq, kp = ["%s%d" % (n, t) for n in ("yt", "yq", "yp", "zq", "zp", "kq", "kp")]
        av, mx = "av%d" % t, "mx%d" % t

        def L(k):
            return rg(lr, 32 * k, 32 * k + 32)

        for k in range(N):
            for dsts in PAR["lists"][k]:
                if r in dsts:
                    lands.append(("lst%d_%d" % (t, k), len(list_engines(k, dsts)[core]), [L(k)]))
        ne = full(prv, r)[1]
        zrun = runs(PAR["ycut"][prv])
        for h, (a, b) in enumerate(zrun):
            if not PAR["whole"][prv]:
                lands.append(("dat%d_%d" % (t, h), 2 * ne, [rg(zq, a, b), rg(zp, a, b)]))
            elif h < len(zrun) - 1:
                lands.append(("dat%d_%d" % (t, h), ne, [rg(zq, a, b)]))
            else:
                lands.append(("dat%d_%d" % (t, h), 2 * ne, [rg(zq, a, b), rg(zp)]))

        for i, (a, b) in enumerate(runs(xcut[t])):
            mm("ms%d" % i, i, "uq2", "us2", 0, xq, xs, a, b)
            mm("mt%d" % i, 4 + i, "uq2", "us2", 0, xq, xs, a, b)
            move("sv%d" % i, "av", rg("sv", a, b), rg("ps%d" % i, 0, b - a))
            move("nv%d" % i, "va", rg("nv", a, b), rg("ps%d" % (4 + i), 0, b - a), mul=-1.0)
        for i, (a, b) in enumerate(runs(PAR["vcut"])):
            tt("vb%d" % i, rg("vb", a, b), rg("sv"), rg("nv", a, b), AluOpType.is_gt, sub(rg("pro"), a, b))
        wrap("wb", "wb", "vb", "kk16", runs(PAR["vcut"]), 128, 3)
        scan("cw", rg("cw"), rg("wb", 13, 3 * C, 16), rg("e3"), MUL, ADD)

        def cw(p0=0, p1=128):
            return rg("cw", 2, 96, 3, p0, p1)
        move("o0", "v", rg("o0"), cw())
        tr("tm", rg("asm", 64, 96), cw())
        for a in range(3):
            tr("tn%d" % a, rg("asm", 32, 64, 1, 32 * a + 32, 32 * a + 64), cw(32 * a, 32 * a + 32))
        tr("to", rg("asm", 0, 32, 1, 64, 128), cw(0, 64))
        for i in range(3):
            tr("b%d" % (i + 1), rg("bt", 32 * i, 32 * i + 32), rg("asm", 48 - 16 * i, 80 - 16 * i))
        move("ou1", "v", rg("ou", 0, 32), rg("bt", 0, 32))
        move("ou2", "v", rg("ou", 32, 96), rg("bt", 32, 96))

        W = runs(PAR["wcut"])
        compose("g1", "r1", "row", rg("o0"), ((0, C),))
        compose("g2", "r2", "r1", rg("ou", 0, 32))
        compose("g3", "r3", "r2", rg("ou", 32, 64))
        compose("g4", "r4", "r3", rg("ou", 64, 96), W)
        wrap("s1", "s1", "r4", "kk16", W, 64)
        for i, (a, b) in enumerate(W):
            ts("o4%d" % i, rg("o4", a // 16, b // 16, 1, 64, 128), rg("s1", a + 15, b, 16, 0, 64), col("fx", 1, 0, 64), ADD)
        compose("g5", "r5", "r4", rg("o4"), W)
        if four:
            wrap("s4", "s4", "r5", "kk4", W)
            for i, (a, b) in enumerate(W):
                ts("of%d" % i, rg(off, a // 4, b // 4), rg("s4", a + 3, b, 4), 4.0, MUL, col("fx", 3), ADD)
        else:
            wrap("s4", "s4", "r5", "kk16", W)
            for k in range(4):
                ts("of%d" % k, rg(off, 32 * k, 32 * k + 32), rg("s4", 15, C, 16), 4.0, MUL, col("f4", k), ADD)
            tr("la", rg("sa", 0, 32, 1, 96, 128), rg("s4", 15, C, 16, 96, 128))
            move("lb", "v", rg("sa", 0, 16, 1, 96, 128), rg("sa", 16, 32, 1, 96, 128))
            for q in (2, 3):
                tr("lc%d" % q, rg("sc", 0, 32, 1, 32 * q, 32 * q + 32), rg("sa", 0, 32, 1, 96, 128))
            for q in range(2):
                ts("lr%d" % q, rg(lr, 32 * r, 32 * r + 32, 1, 64 * q, 64 * q + 64), rg("sc", 0, 32, 1, 64, 128), col("fx", 1, 64, 128), ADD)
        for i, dsts in enumerate(PAR["lists"][r]):
            em, trs = list_engines(r, dsts), []
            for d in dsts:
                rid, pid, _ = topo.addr(cores[d])
                trs.append(RemoteDMATransfer(dst_ids=[DstId(rid=rid, pnc=pid)], dma_engine_mask=sum(1 << e for e in em[cores[d]]),
                                             remote_sem=T.sem["lst%d_%d" % (t, r)], src=ap(L(r)), dst=ap(L(r))))
            op("sl%d" % i, "g", lambda q, trs=trs: g.remote_dma_fused(trs, local_sem=T.sem.sent), [L(r)], [],
               ("far", sum(len(e) for e in em.values())))

        rid, pid, _ = topo.addr(cores[nxt])
        msk, ne = full(r, nxt)

        def send(name, out, in_, h, codes):
            o, i = (ap(out).bitcast(dt.uint8), ap(in_).bitcast(dt.uint8)) if codes else (ap(out), ap(in_))
            sem = T.sem["dat%d_%d" % (t, h)]
            op(name, "g", lambda q, pid=pid, rid=rid, msk=msk: g.remote_dma(o, i, sem, T.sem.sent, pid, rid, msk), [in_], [], ("far", ne))

        yrun = runs(PAR["ycut"][r])
        for h, (a, b) in enumerate(yrun):
            if four:
                m = 4 * a + 32 * ((b - a) * PAR["yshare"] // 256)
                for i, (c, d) in enumerate(((4 * a, m), (m, 4 * b))):
                    move("y%d%d" % (h, i), "av", rg(Y, c, d), rg(X), sub(rg(off), c, d))
            else:
                for i in range(4):
                    move("y%d%d" % (h, i), "av", rg(Y, 4 * a + i, 4 * b, 4), rg(X), sub(rg(off, 32 * i), a, b))
            quant("qy%d" % h, yq, yp, Y, a, b)
            send("sq%d" % h, rg(zq, a, b), rg(yq, a, b), h, True)
            if not PAR["whole"][r]:
                send("sp%d" % h, rg(zp, a, b), rg(yp, a, b), h, False)
            elif h == len(yrun) - 1:
                send("sp%d" % h, rg(zp), rg(yp), h, False)

        sets = [1]

        def banks():
            sets[0] += 1
            return 4 * (sets[0] % 2)

        def vprod(h, q_, p_, a, b):
            k = banks()
            for i in range(4):
                mm("mv%d%d" % (h, i), k + i, "vq", "vp", 128 * i, q_, p_, a, b)
                move("av%d%d" % (h, i), "av", rg(av, C * i + a, C * i + b), rg("ps%d" % (k + i), 0, b - a))

        back = None
        if r == 0:
            for h, (a, b) in enumerate(HALVES):
                vprod(h, yq, yp, a, b)
            compose("La", "la", "row", L(2))
            compose("Lb", "lb", "la", L(1))
            compose("Lc", "lc", "lb", L(0), runs(PAR["bcut"]))
            wrap("s2", "s2", "lc", "kk16", runs(PAR["bcut"]))
            for i, (a, b) in enumerate(runs(PAR["bcut"])):
                ts("bw%d" % i, rg(bw, a // 16, b // 16), rg("s2", a + 15, b, 16), col("fx", 1), ADD)
            wrun = runs(PAR["kcut"])
            for h, (a, b) in enumerate(wrun):
                pick("pk%d" % h, rg(kq, a, b), rg(kp, a, b), rg(zq), rg(zp), sub(rg(bw), a, b))
            wq_, wp_ = kq, kp
        else:
            for h, (a, b) in enumerate(runs(PAR["pcut"])):
                pick("pk%d" % h, rg(kq, a, b), rg(kp, a, b), rg(yq), rg(yp), sub(L(r - 1), a, b))
                vprod(h, kq, kp, a, b)
            wq_, wp_, wrun = zq, zp, zrun
            if r == 2:
                back = L(0)
            if r == 3:
                compose("La", "la", "row", L(1))
                compose("Lb", "lb", "la", L(0))
                back = rg(bw)
                if last:
                    wrap("s2", "s2", "lb", "kk16", HALVES)
                    ts("bw", rg(bw, 0, 32), rg("s2", 15, C, 16), col("fx", 1), ADD)
                else:
                    wrap("s2", "s2", "lb", "kk4", HALVES)
                    ts("bw", rg(bw), rg("s2", 3, C, 4), 4.0, MUL, col("fx", 3), ADD)

        planes = back is not None and not four and not last
        for h, (a, b) in enumerate(wrun):
            k = banks()
            for i in range(4):
                mm("mw%d%d" % (h, i), k + i, "wq", "wp", 128 * i, wq_, wp_, a, b)
                o = rg(mx, C * i + a, C * i + b) if planes else rg(mx, 4 * a + i, 4 * b, 4)
                tt("mx%d%d" % (h, i), o, rg("ps%d" % (k + i), 0, b - a), rg(av, C * i + a, C * i + b), AluOpType.max)
        for h, (a, b) in enumerate(runs(xcut[t + 1])):
            if back is None or last:
                for i, (c, d) in enumerate(parts(4 * a, 4 * b, 2)):
                    move("x%d%d" % (h, i), "av", rg(X2, c, d), rg(mx, c, d), mul=SC)
            elif planes:
                for i in range(4):
                    move("x%d%d" % (h, i), "av", rg(X2, 4 * a + i, 4 * b, 4), rg(mx, C * i, C * i + C), sub(back, a, b), mul=SC)
            else:
                for i, (c, d) in enumerate(parts(4 * a, 4 * b, (b - a) // 64)):
                    move("x%d%d" % (h, i), "av", rg(X2, c, d), rg(mx), sub(back, c, d), mul=SC)
            quant("qn%d" % h, xq2, xs2, X2, a, b)

    tag[0] = ""
    if r == 0:
        move("ol", "av", rg("t9"), rg("r5"), add=MID)
    elif r == 1:
        compose("ol", "t9", "r5", L(0), add=MID)
    else:
        compose("ok", "t8", "r5", L(r - 1))
        compose("ol", "t9", "t8", back, add=MID)
    dma("dl", "sa", "outs", T.ol[:, :], T.t9[0:128:16, :], [rg("t9")], [])
    xq, xs, orun = "xq%d" % R, "xs%d" % R, runs(xcut[R])
    if back is not None:
        orun = runs(PAR["fcut"])
        for h, (a, b) in enumerate(orun):
            pick("pf%d" % h, rg("fq", a, b), rg("fp", a, b), rg(xq), rg(xs), sub(back, a, b))
        xq, xs = "fq", "fp"
    for h, (a, b) in enumerate(orun):
        bank = 4 * (h % 2) + h // 2
        mm("my%d" % h, bank, "aq", "asc", 0, xq, xs, a, b)
        dma("dc%d" % h, "sa", "outs", T.oc[:, 4 * a:4 * b], ap(rg(xq, a, b)).bitcast(dt.uint8), [rg(xq, a, b)], [])
        move("ys%d" % h, "va", rg("ysb", a, b), rg("ps%d" % bank, 0, b - a))
        dma("dy%d" % h, "sa", "outs", T.y[:, a:b], ap(rg("ysb", a, b)), [rg("ysb", a, b)], [])
    for k in range(4):
        dma("ds%d" % k, "sa", "outs", T.osc[4 * k:4 * k + 4, :], T[xs][32 * k:32 * k + 4, :], [rg(xs)], [])
    return calls, lands


def merge(calls, lines):
    seen, need = {}, {}
    for name, qs, kind, fn, reads, writes in calls:
        need[name] = {m for y, w in [(y, True) for y in writes] + [(y, False) for y in reads] for x, wr, m in seen.get(y[0], [])
                      if (w or wr or x[0].startswith("ps")) and meet(x, y)}
        for x in reads:
            seen.setdefault(x[0], []).append((x, False, name))
        for x in writes:
            seen.setdefault(x[0], []).append((x, True, name))
    todo = {q: lines[q].split() for q in lines}
    seq, done = [], set()
    while any(todo.values()):
        free = [q for q in todo if todo[q] and need[todo[q][0]] <= done]
        assert free
        for q in free:
            done.add(todo[q][0])
            seq.append((todo[q].pop(0), q))
    assert done == set(need) and len(seq) == len(calls)
    return seq


def rank_program(g, core, T, topo):
    r = T.rank_of(core)
    if r is None:
        return
    Q = {"v": g.vector, "a": g.scalar, "p": g.tensor, "s": g.sync, "g": g}
    CS = {"v": "cv", "a": "ca", "p": "cp", "g": "cg"}
    cnt, known, waited, hist = {}, {q: {} for q in Q}, {}, {}
    calls, lands = plan(g, core, T, topo)

    def wait(q, ev):
        sem, n, clock = ev
        if known[q].get(sem, 0) >= n:
            return
        Q[q].wait_ge(T.sem[sem], n)
        waited[sem] = max(waited.get(sem, 0), n)
        for k, v in clock.items():
            known[q][k] = max(known[q].get(k, 0), v)
        known[q][sem] = n

    def order(q, reads, writes):
        need = {}
        for y, w in [(y, True) for y in writes] + [(y, False) for y in reads]:
            for x, wr, ev, eq in hist.get(y[0], []):
                if (w or wr or (x[0].startswith("ps") and eq != q)) and meet(x, y) and (ev[0] not in need or need[ev[0]][1] < ev[1]):
                    need[ev[0]] = ev
        evs = list(need.values())
        for ev in evs:
            if not any(o is not ev and o[2].get(ev[0], 0) >= ev[1] for o in evs):
                wait(q, ev)

    def note(q, ev, reads, writes):
        for x in reads:
            hist.setdefault(x[0], []).append((x, False, ev, q))
        for x in writes:
            hist.setdefault(x[0], []).append((x, True, ev, q))

    for sem, n, writes in lands:
        cnt[sem] = n
        note("far", (sem, n, {}), [], writes)

    byname = {c[0]: c for c in calls}
    for name, q in merge(calls, ORDER[r]):
        _, qs, kind, fn, reads, writes = byname[name]
        assert q in qs
        order(q, reads, writes)
        if kind[0] == "far":
            fn(q)
            cnt["sent"] = cnt.get("sent", 0) + kind[1]
            continue
        sem, n = (CS[q], 1) if kind == "op" else (kind[1], 16)
        fn(q).then_inc(T.sem[sem], n)
        cnt[sem] = cnt.get(sem, 0) + n
        note(q, (sem, cnt[sem], dict(known[q])), reads, writes)

    for sem in sorted(cnt, key=lambda k: k == "outs"):
        if waited.get(sem, 0) < cnt[sem]:
            g.wait_ge(T.sem[sem], cnt[sem])
